import numpy as np
import ml_dtypes


def mxq(x, axis, fmt="e4m3"):
    dtype, down = {"e4m3": (ml_dtypes.float8_e4m3fn, 7), "e5m2": (ml_dtypes.float8_e5m2, 14)}[fmt]
    v = np.moveaxis(np.asarray(x, np.float32).astype(ml_dtypes.bfloat16).astype(np.float64), axis, -1)
    blocks = v.reshape(v.shape[:-1] + (-1, 32))
    amax = np.abs(blocks).max(-1, keepdims=True)
    byte = np.maximum(np.where(amax > 0, np.frexp(amax)[1] - 1 + 127, 0) - down, 1)
    scale = np.exp2(byte - 127.0)
    codes = (blocks / scale).astype(np.float32).astype(dtype).astype(np.float64)
    return np.moveaxis((codes * scale).reshape(v.shape), -1, axis)


WIDE = False


def mx_kscale(k):
    if not WIDE:
        return np.ones(k)
    levels = np.array([24, -24, 12, -12, 0])
    if k % 512:
        return np.exp2(np.random.permutation(np.resize(levels, k // 32))).repeat(32)
    a = np.empty((k // 512, 16))
    for p in range(k // 512):
        a[p, :8] = np.random.permutation(np.resize(levels, 8))
        for g in range(8):
            far = levels[np.abs(levels - a[p, g]) >= 10]
            a[p, g + 8] = far[np.random.randint(len(far))]
    return np.exp2(a.ravel()).repeat(32)


def f64(x):
    return np.asarray(x).astype(np.float64)


def striped(idx):
    return np.tile(idx.reshape(-1, 16).T, (8, 1)).astype(np.uint16)


def unstriped(offs):
    return offs[:16].T.reshape(-1).astype(np.int64)


E2M1 = np.array([0.0, 0.5, 1.0, 1.5, 2.0, 3.0, 4.0, 6.0, -0.0, -0.5, -1.0, -1.5, -2.0, -3.0, -4.0, -6.0])


def pack_weight(w, fmt):
    k, n = w.shape
    w = f64(np.asarray(w, np.float32).astype(ml_dtypes.bfloat16)).reshape(k // 32, 32, n)
    amax = np.abs(w).max(1)
    if fmt == "e4m3":
        byte = np.frexp(amax)[1] - 1 + 127 - 7
    else:
        mant, ex = np.frexp(amax / 6.0)
        byte = np.where(mant > 0.5, ex, ex - 1) + 127
    byte = np.clip(np.where(amax > 0, byte, 1), 1, 254)
    scaled = (w * np.exp2(127.0 - byte)[:, None, :]).reshape(k, n).astype(np.float32)
    by_word = np.ascontiguousarray(scaled.reshape(k // 512, 128, 4, n).transpose(0, 1, 3, 2))
    if fmt == "e4m3":
        words = by_word.astype(ml_dtypes.float8_e4m3fn).view(np.uint8)
    else:
        c = by_word.astype(ml_dtypes.float4_e2m1fn).view(np.uint8) & 0xF
        words = (c[..., 0::2] | (c[..., 1::2] << 4)).reshape(k // 512, 128, 2 * n)
    return np.ascontiguousarray(words), np.ascontiguousarray(byte.astype(np.uint8).reshape(k // 512, 16, n))


def unpack_weight(words, scales, fmt):
    g, _, n = scales.shape
    words = np.ascontiguousarray(words).reshape(g, 128, n, -1)
    if fmt == "e4m3":
        vals = words.view(ml_dtypes.float8_e4m3fn).astype(np.float64)
    else:
        nib = np.empty((g, 128, n, 4), np.uint8)
        nib[..., 0::2] = words & 0xF
        nib[..., 1::2] = words >> 4
        vals = E2M1[nib]
    vals = vals * np.repeat(np.exp2(scales.astype(np.float64) - 127.0), 8, axis=1)[..., None]
    return vals.transpose(0, 1, 3, 2).reshape(g * 512, n)


K, L, R, N, T, J = 512, 512, 1024, 256, 4096, 2048


def setup_inputs():
    n = np.random.standard_normal
    s = mx_kscale(K)[:, None]
    s2 = mx_kscale(L)[:, None]
    u = mx_kscale(R)[:, None]
    p_tab = pack_weight(n((K, T)) * s, "e4m3")
    p_tab2 = pack_weight(n((L, T)) * s2, "e4m3")
    p_wb = pack_weight(n((L, R)) / np.sqrt(L) / s2, "e4m3")
    p_en = pack_weight(n((R, N)) / np.sqrt(R) / u, "e2m1")
    return {
        "tab_words": p_tab[0],
        "tab_scales": p_tab[1],
        "tab2_words": p_tab2[0],
        "tab2_scales": p_tab2[1],
        "wa": (n((K, R)) / np.sqrt(K) / s).astype(np.float32),
        "wb_words": p_wb[0],
        "wb_scales": p_wb[1],
        "sm": (np.random.uniform(0.5, 2.0, R) * u[:, 0]).astype(np.float32),
        "en_words": p_en[0],
        "en_scales": p_en[1],
        "b": (0.3 * n(N)).astype(np.float32),
        "offs": striped(np.random.permutation(T)[:J]),
        "offs2": striped(np.random.permutation(T)[:J]),
    }


def reference(tab_words, tab_scales, tab2_words, tab2_scales, wa, wb_words, wb_scales, sm, en_words, en_scales, b, offs, offs2):
    idx = unstriped(offs)
    idx2 = unstriped(offs2)
    tab_ = unpack_weight(tab_words, tab_scales, "e4m3")[:, idx]
    tab2_ = unpack_weight(tab2_words, tab2_scales, "e4m3")[:, idx2]
    wa_ = mxq(f64(wa), 0, "e4m3")
    wb_ = unpack_weight(wb_words, wb_scales, "e4m3")
    ha = wa_.T @ tab_
    hb = wb_.T @ tab2_
    h = f64(sm)[:, None] * (ha - hb) ** 2
    h_ = mxq(h, 0, "e4m3")
    en_ = unpack_weight(en_words, en_scales, "e2m1")
    y = en_.T @ h_
    return y + f64(b)[:, None]

@@ -1,0 +1,245 @@
+from contextlib import ExitStack
+
+import concourse.mybir as mybir
+
+K, L, R, N, T, J = 512, 512, 1024, 256, 4096, 2048
+FLOPS = 2 * K * R * J + 2 * L * R * J + 2 * R * N * J
+
+F32 = mybir.dt.float32
+BF16 = mybir.dt.bfloat16
+I32 = mybir.dt.int32
+U32 = mybir.dt.uint32
+U16 = mybir.dt.uint16
+U8 = mybir.dt.uint8
+FP8X4 = mybir.dt.float8_e4m3fn_x4
+FP4X4 = mybir.dt.float4_e2m1fn_x4
+ACT = mybir.ActivationFunctionType
+ALU = mybir.AluOpType
+
+P = 128
+PACK = 4
+KP = P * PACK
+HALVES = R // KP
+CH = 512
+NCH = J // CH
+LISTCOLS = CH // 16
+NT = N // P
+
+
+def tile_list_kg_sqd_bias_kernel(
+    tc, tab_words, tab_scales, tab2_words, tab2_scales, wa, wb_words, wb_scales, sm, en_words, en_scales, b, offs, offs2, out
+):
+    nc = tc.nc
+    with ExitStack() as ctx:
+        lists = ctx.enter_context(tc.tile_pool(name="lists", bufs=1))
+        keep = ctx.enter_context(tc.tile_pool(name="keep", bufs=1))
+        loads = ctx.enter_context(tc.tile_pool(name="loads", bufs=1))
+        ring = ctx.enter_context(tc.tile_pool(name="ring", bufs=2))
+        psum = ctx.enter_context(tc.psum_pool(name="psum", bufs=1))
+
+        offs_t = lists.tile([P, J // 16], U16, name="offs_t")
+        offs2_t = lists.tile([P, J // 16], U16, name="offs2_t")
+        tabs = keep.tile([P, T], U8, name="tabs", align_bytes=64)
+        tab2s = keep.tile([P, T], U8, name="tab2s", align_bytes=64)
+        wbs_raw = keep.tile([P, R], U8, name="wbs_raw", align_bytes=64)
+        ens = keep.tile([P, HALVES, N], U8, name="ens", align_bytes=64)
+        WORDS = 2 * T + 2 * PACK * KP + R + HALVES * N // 2 + 16
+        zeros = loads.tile([P, WORDS], I32, name="zeros", offset=0)
+        nc.vector.memset(tabs[:].bitcast(I32), 0)
+        nc.gpsimd.memset(tab2s[:].bitcast(I32), 0)
+        nc.vector.memset(zeros[:, 0:1], 0)
+        nc.vector.tensor_copy(out=wbs_raw[:].bitcast(I32), in_=zeros[:, 0:1].to_broadcast([P, R // 4]))
+        nc.gpsimd.memset(ens[:].rearrange("p a n -> p (a n)").bitcast(I32), 0)
+
+        wa_rows = wa.rearrange("(p i) r -> p i r", i=PACK)
+        wb_flat = wb_words[0].rearrange("p r i -> p (r i)")
+        tabw = loads.tile([P, T], U32, name="tabw", align_bytes=64, offset=0)
+        tab2w = loads.tile([P, T], U32, name="tab2w", align_bytes=64, offset=4 * T)
+        wa_raw = [loads.tile([P, PACK, KP], F32, name="wa_raw%d" % a, offset=8 * T + 4 * PACK * KP * a) for a in range(HALVES)]
+        wb_raw = loads.tile([P, R], I32, name="wb_raw", align_bytes=64, offset=8 * T + 8 * PACK * KP)
+        enw = loads.tile([P, HALVES, 2 * N], U8, name="enw", align_bytes=64, offset=8 * T + 8 * PACK * KP + 4 * R)
+        b_t = loads.tile([P, NT], F32, name="b_t", offset=8 * T + 8 * PACK * KP + 4 * R + HALVES * 2 * N)
+        sm_t = loads.tile([P, HALVES, PACK], F32, name="sm_t", offset=8 * T + 8 * PACK * KP + 4 * R + HALVES * 2 * N + 32)
+
+        nc.sync.dma_start(offs_t[:], offs)
+        for q in range(4):
+            nc.sync.dma_start(out=tabs[32 * q : 32 * q + 4, :].bitcast(I32), in_=tab_scales[0, 4 * q : 4 * q + 4, :].bitcast(I32))
+        nc.sync.dma_start(offs2_t[:], offs2)
+        nc.sync.dma_start(out=wa_raw[0][:], in_=wa_rows[:, :, 0:KP])
+        nc.sync.dma_start(out=sm_t[:], in_=sm.rearrange("(a p t) -> p a t", a=HALVES, t=PACK))
+        for q in range(4):
+            nc.sync.dma_start(out=tab2s[32 * q : 32 * q + 4, :].bitcast(I32), in_=tab2_scales[0, 4 * q : 4 * q + 4, :].bitcast(I32))
+        nc.sync.dma_start(out=wb_raw[:], in_=wb_flat.bitcast(I32))
+        for q in range(4):
+            nc.sync.dma_start(out=wbs_raw[32 * q : 32 * q + 4, :].bitcast(I32), in_=wb_scales[0, 4 * q : 4 * q + 4, :].bitcast(I32))
+        nc.sync.dma_start(out=tabw[:].bitcast(I32), in_=tab_words[0].rearrange("p t i -> p (t i)").bitcast(I32))
+        nc.sync.dma_start(out=tab2w[:].bitcast(I32), in_=tab2_words[0].rearrange("p t i -> p (t i)").bitcast(I32))
+        nc.sync.dma_start(out=wa_raw[1][:], in_=wa_rows[:, :, KP:R])
+        nc.sync.dma_start(out=enw[:].bitcast(I32), in_=en_words.rearrange("a p n -> p a n").bitcast(I32))
+        for q in range(4):
+            nc.sync.dma_start(
+                out=ens[32 * q : 32 * q + 4, :, :].bitcast(I32),
+                in_=en_scales[:, 4 * q : 4 * q + 4, :].rearrange("a q n -> q a n").bitcast(I32),
+            )
+        with nc.allow_non_contiguous_dma(reason="one bias value a partition"):
+            nc.sync.dma_start(out=b_t[:], in_=b.rearrange("(c p) -> p c", p=P))
+
+        W = HALVES * PACK
+        smf = sm_t[:].rearrange("p a t -> p (a t)")
+        sgn = keep.tile([P, W], F32, name="sgn")
+        mag = keep.tile([P, W], F32, name="mag")
+        guess = keep.tile([P, W], F32, name="guess")
+        guess_sq = keep.tile([P, W], F32, name="guess_sq")
+        half_inv = keep.tile([P, W], F32, name="half_inv")
+        resid = keep.tile([P, W], F32, name="resid")
+        root = keep.tile([P, W], F32, name="root")
+        nc.scalar.activation(out=half_inv[:], in_=smf, func=ACT.Abs_reciprocal_sqrt, scale=4.0)
+        nc.scalar.activation(out=mag[:], in_=smf, func=ACT.Abs)
+        nc.scalar.activation(out=guess[:], in_=mag[:], func=ACT.Sqrt)
+        nc.scalar.activation(out=sgn[:], in_=smf, func=ACT.Sign)
+        nc.scalar.activation(out=guess_sq[:], in_=guess[:], func=ACT.Square)
+        nc.gpsimd.tensor_tensor(resid[:], mag[:], guess_sq[:], ALU.subtract)
+        nc.gpsimd.tensor_scalar(half_inv[:], half_inv[:], 2.0**62, 1.0, ALU.min, ALU.mult)
+        nc.gpsimd.tensor_tensor(resid[:], resid[:], half_inv[:], ALU.mult)
+        nc.gpsimd.tensor_tensor(root[:], guess[:], resid[:], ALU.add)
+
+        wa_codes = [keep.tile([P, KP], U32, name="wa_codes%d" % a, align_bytes=64) for a in range(HALVES)]
+        wa_scales = [keep.tile([P, KP], U8, name="wa_scales%d" % a, align_bytes=64) for a in range(HALVES)]
+        wb_codes = keep.tile([P, R], I32, name="wb_codes", align_bytes=64)
+        wbs = keep.tile([P, R], U8, name="wbs", align_bytes=64)
+
+        def prepare_wa(a):
+            wa_bf = keep.tile([P, PACK, P, PACK], BF16, name="wa_bf%d" % a, align_bytes=64)
+            nc.scalar.activation(
+                out=wa_bf[:].rearrange("p t m i -> p m i t"),
+                in_=wa_raw[a][:].rearrange("p i (m t) -> p m i t", t=PACK),
+                func=ACT.Copy,
+                scale=-1.0,
+            )
+            nc.vector.quantize_mx(out=wa_codes[a][:].bitcast(FP8X4), scales=wa_scales[a][:], in_=wa_bf[:].rearrange("p t m i -> p (t m i)"))
+
+        def prepare_wb():
+            nc.vector.tensor_copy(
+                out=wb_codes[:].rearrange("p (a t m) -> p a m t", a=HALVES, t=PACK),
+                in_=wb_raw[:].rearrange("p (a m t) -> p a m t", a=HALVES, t=PACK),
+            )
+            nc.vector.tensor_copy(
+                out=wbs[:].rearrange("p (a t m) -> p a m t", a=HALVES, t=PACK),
+                in_=wbs_raw[:].rearrange("p (a m t) -> p a m t", a=HALVES, t=PACK),
+            )
+
+        picked = {}
+
+        def gather(kind, c):
+            table, offsets, dtype, bufs = {
+                "s1": (tabs, offs_t, U8, 3),
+                "s2": (tab2s, offs2_t, U8, 3),
+                "w1": (tabw, offs_t, U32, 2),
+                "w2": (tab2w, offs2_t, U32, 2),
+            }[kind]
+            dst = ring.tile([P, CH], dtype, name="picked_" + kind, bufs=bufs, align_bytes=64)
+            nc.vector.tensor_copy(dst[:], table[:].indirect(offsets[:, c * LISTCOLS : (c + 1) * LISTCOLS]))
+            picked[(kind, c)] = dst
+
+        planes, woven, hq = {}, {}, {}
+
+        def stage1(j0, width, a):
+            c = j0 // CH
+            js = slice(j0 - c * CH, j0 - c * CH + width)
+            pl = ring.tile([P, PACK, width], BF16, name="planes", bufs=3, align_bytes=64)
+            planes[(j0, a)] = pl
+            for t in range(PACK):
+                bank = psum.tile([P, width], F32, name="dbank", bufs=6)
+                cols = slice(t * P, (t + 1) * P)
+                wcols = slice(a * KP + t * P, a * KP + (t + 1) * P)
+                nc.tensor.matmul_mx(
+                    out=bank[:], lhsT=wa_codes[a][:, cols].bitcast(FP8X4), lhsT_scale=wa_scales[a][:, cols],
+                    rhs=picked[("w1", c)][:, js].bitcast(FP8X4), rhs_scale=picked[("s1", c)][:, js], start=True, stop=False,
+                )
+                nc.tensor.matmul_mx(
+                    out=bank[:], lhsT=wb_codes[:, wcols].bitcast(FP8X4), lhsT_scale=wbs[:, wcols],
+                    rhs=picked[("w2", c)][:, js].bitcast(FP8X4), rhs_scale=picked[("s2", c)][:, js], start=False, stop=True,
+                )
+                u = a * PACK + t
+                nc.scalar.activation(out=pl[:, t, :], in_=bank[:], func=ACT.Square, scale=root[:, u : u + 1])
+
+        def signs(j0, width, a):
+            pl = planes[(j0, a)]
+            for t in range(PACK):
+                u = a * PACK + t
+                nc.vector.tensor_scalar(pl[:, t, :], pl[:, t, :], sgn[:, u : u + 1], None, ALU.mult)
+
+        def weave(j0, width, a, on_scalar):
+            wv = ring.tile([P, width, PACK], BF16, name="woven", bufs=3, align_bytes=64)
+            woven[(j0, a)] = wv
+            dst = wv[:].rearrange("p (g i) t -> p g t i", i=4)
+            src = planes[(j0, a)][:].rearrange("p t (g i) -> p g t i", i=4)
+            if on_scalar:
+                nc.scalar.copy(out=dst, in_=src)
+            else:
+                nc.vector.tensor_copy(out=dst, in_=src)
+
+        def quantise(j0, width, a):
+            codes = ring.tile([P, width], U32, name="h_codes", bufs=3, align_bytes=64)
+            scales = ring.tile([P, width], U8, name="h_scales", bufs=3, align_bytes=64)
+            hq[(j0, a)] = (codes, scales)
+            nc.vector.quantize_mx(out=codes[:].bitcast(FP8X4), scales=scales[:], in_=woven[(j0, a)][:].rearrange("p j t -> p (j t)"))
+
+        def stage2(j0, width):
+            run = CH if width == CH else P
+            for nt in range(NT):
+                ybank = psum.tile([P, width], F32, name="ybank", bufs=2)
+                for a in range(HALVES):
+                    codes, scales = hq[(j0, a)]
+                    for s in range(0, width, run):
+                        nc.tensor.matmul_mx(
+                            out=ybank[:, s : s + run],
+                            lhsT=enw[:, a, 2 * nt * P : 2 * (nt + 1) * P].bitcast(FP4X4),
+                            lhsT_scale=ens[:, a, nt * P : (nt + 1) * P],
+                            rhs=codes[:, s : s + run].bitcast(FP8X4),
+                            rhs_scale=scales[:, s : s + run],
+                            start=(a == 0 and s == 0),
+                            stop=(a == HALVES - 1 and s + run == width),
+                        )
+                y = ring.tile([P, width], F32, name="y", bufs=4)
+                if j0 + width == J and nt == NT - 1:
+                    nc.vector.tensor_scalar(y[:], ybank[:], b_t[:, nt : nt + 1], None, ALU.add)
+                else:
+                    nc.scalar.activation(out=y[:], in_=ybank[:], func=ACT.Identity, bias=b_t[:, nt : nt + 1])
+                nc.sync.dma_start(out=out[nt * P : (nt + 1) * P, j0 : j0 + width], in_=y[:])
+
+        for c in range(3):
+            gather("s1", c)
+        for c in range(3):
+            gather("s2", c)
+        prepare_wb()
+        prepare_wa(0)
+        gather("w1", 0)
+        gather("w1", 1)
+        gather("w2", 0)
+        gather("w2", 1)
+        prepare_wa(1)
+
+        pieces = [(0, CH), (CH, CH), (2 * CH, CH), (3 * CH, CH // 2), (3 * CH + CH // 2, CH // 2)]
+        units = [(j0, width, a) for (j0, width) in pieces for a in range(HALVES)]
+        SCALAR_WEAVES = (1, 3)
+        for u in range(len(units) + 2):
+            if u < len(units):
+                stage1(*units[u])
+                signs(*units[u])
+            if 1 <= u <= len(units):
+                weave(*units[u - 1], u - 1 in SCALAR_WEAVES)
+            if u < len(units):
+                j0, width, a = units[u]
+                c = j0 // CH
+                if a == 1 and c + 2 < NCH:
+                    gather("w1", c + 2)
+                    gather("w2", c + 2)
+                if a == 1 and c + 3 < NCH:
+                    gather("s1", c + 3)
+                    gather("s2", c + 3)
+            if u >= 2:
+                j0, width, a = units[u - 2]
+                quantise(j0, width, a)
+                if a == 1:
+                    stage2(j0, width)

@@ -43,8 +43,15 @@ def tile_list_kg_sqd_bias_kernel(
         tab2s = keep.tile([P, T], U8, name="tab2s", align_bytes=64)
         wbs_raw = keep.tile([P, R], U8, name="wbs_raw", align_bytes=64)
         ens = keep.tile([P, HALVES, N], U8, name="ens", align_bytes=64)
-        WORDS = 2 * T + 2 * PACK * KP + R + HALVES * N // 2 + 16
-        zeros = loads.tile([P, WORDS], I32, name="zeros", offset=0)
+        HALF_BYTES = 4 * PACK * KP
+        at_wa = 8 * T
+        at_wb = at_wa + HALVES * HALF_BYTES
+        at_en = at_wb + 4 * KP
+        at_b = at_en + HALVES * 2 * N
+        at_sm = at_b + 64
+        at_mid = at_sm + 64
+        at_last = at_mid + 8 * CH
+        zeros = loads.tile([P, at_last // 4], I32, name="zeros", offset=0)
         nc.vector.memset(tabs[:].bitcast(I32), 0)
         nc.gpsimd.memset(tab2s[:].bitcast(I32), 0)
         nc.vector.memset(zeros[:, 0:1], 0)
@@ -52,14 +59,14 @@ def tile_list_kg_sqd_bias_kernel(
         nc.gpsimd.memset(ens[:].rearrange("p a n -> p (a n)").bitcast(I32), 0)
 
         wa_rows = wa.rearrange("(p i) r -> p i r", i=PACK)
-        wb_flat = wb_words[0].rearrange("p r i -> p (r i)")
+        wb_flat = wb_words[0].rearrange("p r i -> p (r i)").bitcast(I32)
         tabw = loads.tile([P, T], U32, name="tabw", align_bytes=64, offset=0)
         tab2w = loads.tile([P, T], U32, name="tab2w", align_bytes=64, offset=4 * T)
-        wa_raw = [loads.tile([P, PACK, KP], F32, name="wa_raw%d" % a, offset=8 * T + 4 * PACK * KP * a) for a in range(HALVES)]
-        wb_raw = loads.tile([P, R], I32, name="wb_raw", align_bytes=64, offset=8 * T + 8 * PACK * KP)
-        enw = loads.tile([P, HALVES, 2 * N], U8, name="enw", align_bytes=64, offset=8 * T + 8 * PACK * KP + 4 * R)
-        b_t = loads.tile([P, NT], F32, name="b_t", offset=8 * T + 8 * PACK * KP + 4 * R + HALVES * 2 * N)
-        sm_t = loads.tile([P, HALVES, PACK], F32, name="sm_t", offset=8 * T + 8 * PACK * KP + 4 * R + HALVES * 2 * N + 32)
+        wa_raw = [loads.tile([P, PACK, KP], F32, name="wa_raw%d" % a, offset=at_wa + HALF_BYTES * a) for a in range(HALVES)]
+        wb_raw = [loads.tile([P, KP], I32, name="wb_raw%d" % a, offset=(at_wb, at_mid)[a]) for a in range(HALVES)]
+        enw = loads.tile([P, HALVES, 2 * N], U8, name="enw", align_bytes=64, offset=at_en)
+        b_t = loads.tile([P, NT], F32, name="b_t", offset=at_b)
+        sm_t = loads.tile([P, HALVES, PACK], F32, name="sm_t", offset=at_sm)
 
         nc.sync.dma_start(offs_t[:], offs)
         for q in range(4):
@@ -69,11 +76,12 @@ def tile_list_kg_sqd_bias_kernel(
         nc.sync.dma_start(out=sm_t[:], in_=sm.rearrange("(a p t) -> p a t", a=HALVES, t=PACK))
         for q in range(4):
             nc.sync.dma_start(out=tab2s[32 * q : 32 * q + 4, :].bitcast(I32), in_=tab2_scales[0, 4 * q : 4 * q + 4, :].bitcast(I32))
-        nc.sync.dma_start(out=wb_raw[:], in_=wb_flat.bitcast(I32))
+        nc.sync.dma_start(out=wb_raw[0][:], in_=wb_flat[:, 0:KP])
         for q in range(4):
             nc.sync.dma_start(out=wbs_raw[32 * q : 32 * q + 4, :].bitcast(I32), in_=wb_scales[0, 4 * q : 4 * q + 4, :].bitcast(I32))
         nc.sync.dma_start(out=tabw[:].bitcast(I32), in_=tab_words[0].rearrange("p t i -> p (t i)").bitcast(I32))
         nc.sync.dma_start(out=tab2w[:].bitcast(I32), in_=tab2_words[0].rearrange("p t i -> p (t i)").bitcast(I32))
+        nc.sync.dma_start(out=wb_raw[1][:], in_=wb_flat[:, KP:R])
         nc.sync.dma_start(out=wa_raw[1][:], in_=wa_rows[:, :, KP:R])
         nc.sync.dma_start(out=enw[:].bitcast(I32), in_=en_words.rearrange("a p n -> p a n").bitcast(I32))
         for q in range(4):
@@ -105,7 +113,7 @@ def tile_list_kg_sqd_bias_kernel(
 
         wa_codes = [keep.tile([P, KP], U32, name="wa_codes%d" % a, align_bytes=64) for a in range(HALVES)]
         wa_scales = [keep.tile([P, KP], U8, name="wa_scales%d" % a, align_bytes=64) for a in range(HALVES)]
-        wb_codes = keep.tile([P, R], I32, name="wb_codes", align_bytes=64)
+        wb_codes = [keep.tile([P, KP], I32, name="wb_codes%d" % a, align_bytes=64) for a in range(HALVES)]
         wbs = keep.tile([P, R], U8, name="wbs", align_bytes=64)
 
         def prepare_wa(a):
@@ -118,79 +126,107 @@ def tile_list_kg_sqd_bias_kernel(
             )
             nc.vector.quantize_mx(out=wa_codes[a][:].bitcast(FP8X4), scales=wa_scales[a][:], in_=wa_bf[:].rearrange("p t m i -> p (t m i)"))
 
-        def prepare_wb():
+        def deal_wb_words(a):
             nc.vector.tensor_copy(
-                out=wb_codes[:].rearrange("p (a t m) -> p a m t", a=HALVES, t=PACK),
-                in_=wb_raw[:].rearrange("p (a m t) -> p a m t", a=HALVES, t=PACK),
+                out=wb_codes[a][:].rearrange("p (t m) -> p m t", t=PACK),
+                in_=wb_raw[a][:].rearrange("p (m t) -> p m t", t=PACK),
             )
+
+        def deal_wb_scales():
             nc.vector.tensor_copy(
                 out=wbs[:].rearrange("p (a t m) -> p a m t", a=HALVES, t=PACK),
                 in_=wbs_raw[:].rearrange("p (a m t) -> p a m t", a=HALVES, t=PACK),
             )
 
         picked = {}
+        last_at = {"w1": at_last, "s1": at_last + 4 * CH, "s2": at_last + 5 * CH, "w2": at_last + 6 * CH}
 
-        def gather(kind, c):
-            table, offsets, dtype, bufs = {
-                "s1": (tabs, offs_t, U8, 3),
-                "s2": (tab2s, offs2_t, U8, 3),
-                "w1": (tabw, offs_t, U32, 2),
-                "w2": (tab2w, offs2_t, U32, 2),
+        def gather(kind, c0, c1):
+            table, offsets, dtype = {
+                "s1": (tabs, offs_t, U8),
+                "s2": (tab2s, offs2_t, U8),
+                "w1": (tabw, offs_t, U32),
+                "w2": (tab2w, offs2_t, U32),
             }[kind]
-            dst = ring.tile([P, CH], dtype, name="picked_" + kind, bufs=bufs, align_bytes=64)
-            nc.vector.tensor_copy(dst[:], table[:].indirect(offsets[:, c * LISTCOLS : (c + 1) * LISTCOLS]))
-            picked[(kind, c)] = dst
+            name = "picked_%s_%d" % (kind, c0)
+            shape = [P, (c1 - c0) * CH]
+            if c0 == NCH - 1:
+                dst = loads.tile(shape, dtype, name=name, align_bytes=64, offset=last_at[kind])
+            elif kind == "w1" and c0 > 0:
+                dst = loads.tile(shape, dtype, name=name, align_bytes=64, offset=at_mid)
+            else:
+                dst = keep.tile(shape, dtype, name=name, align_bytes=64)
+            nc.vector.tensor_copy(dst[:], table[:].indirect(offsets[:, c0 * LISTCOLS : c1 * LISTCOLS]))
+            for c in range(c0, c1):
+                picked[(kind, c)] = dst[:, (c - c0) * CH : (c - c0 + 1) * CH]
 
-        planes, woven, hq = {}, {}, {}
+        banks = [psum.tile([P, CH], F32, name="bank%d" % i) for i in range(8)]
+        turn = []
 
-        def stage1(j0, width, a):
+        def next_bank(width):
+            turn.append(width)
+            return banks[(len(turn) - 1) % 8][:, 0:width]
+
+        pieces = [(0, CH), (CH, CH), (2 * CH, CH), (3 * CH, CH // 2), (3 * CH + CH // 2, CH // 2)]
+        units = [(0, 0), (1, 0), (0, 1), (1, 1)] + [(k, a) for k in range(2, len(pieces)) for a in range(HALVES)]
+        squares, signed, woven, hq = {}, {}, {}, {}
+
+        def stage1(u):
+            k, a = units[u]
+            j0, width = pieces[k]
             c = j0 // CH
             js = slice(j0 - c * CH, j0 - c * CH + width)
-            pl = ring.tile([P, PACK, width], BF16, name="planes", bufs=3, align_bytes=64)
-            planes[(j0, a)] = pl
+            if u == 0:
+                squares[u] = loads.tile([P, PACK, width], BF16, name="squares0", align_bytes=64, offset=at_last + 3 * CH)
+            else:
+                squares[u] = keep.tile([P, PACK, width], BF16, name="squares%d" % u, tag="first%d" % u, align_bytes=64)
             for t in range(PACK):
-                bank = psum.tile([P, width], F32, name="dbank", bufs=6)
+                bank = next_bank(width)
                 cols = slice(t * P, (t + 1) * P)
-                wcols = slice(a * KP + t * P, a * KP + (t + 1) * P)
+                scols = slice(a * KP + t * P, a * KP + (t + 1) * P)
                 nc.tensor.matmul_mx(
-                    out=bank[:], lhsT=wa_codes[a][:, cols].bitcast(FP8X4), lhsT_scale=wa_scales[a][:, cols],
+                    out=bank, lhsT=wa_codes[a][:, cols].bitcast(FP8X4), lhsT_scale=wa_scales[a][:, cols],
                     rhs=picked[("w1", c)][:, js].bitcast(FP8X4), rhs_scale=picked[("s1", c)][:, js], start=True, stop=False,
                 )
                 nc.tensor.matmul_mx(
-                    out=bank[:], lhsT=wb_codes[:, wcols].bitcast(FP8X4), lhsT_scale=wbs[:, wcols],
+                    out=bank, lhsT=wb_codes[a][:, cols].bitcast(FP8X4), lhsT_scale=wbs[:, scols],
                     rhs=picked[("w2", c)][:, js].bitcast(FP8X4), rhs_scale=picked[("s2", c)][:, js], start=False, stop=True,
                 )
-                u = a * PACK + t
-                nc.scalar.activation(out=pl[:, t, :], in_=bank[:], func=ACT.Square, scale=root[:, u : u + 1])
+                col = a * PACK + t
+                nc.scalar.activation(out=squares[u][:, t, :], in_=bank, func=ACT.Square, scale=root[:, col : col + 1])
 
-        def signs(j0, width, a):
-            pl = planes[(j0, a)]
+        def signs(u):
+            k, a = units[u]
+            width = pieces[k][1]
+            signed[u] = keep.tile([P, PACK, width], BF16, name="signed%d" % u, tag="second%d" % u, align_bytes=64)
             for t in range(PACK):
-                u = a * PACK + t
-                nc.vector.tensor_scalar(pl[:, t, :], pl[:, t, :], sgn[:, u : u + 1], None, ALU.mult)
+                col = a * PACK + t
+                nc.vector.tensor_scalar(signed[u][:, t, :], squares[u][:, t, :], sgn[:, col : col + 1], None, ALU.mult)
 
-        def weave(j0, width, a, on_scalar):
-            wv = ring.tile([P, width, PACK], BF16, name="woven", bufs=3, align_bytes=64)
-            woven[(j0, a)] = wv
-            dst = wv[:].rearrange("p (g i) t -> p g t i", i=4)
-            src = planes[(j0, a)][:].rearrange("p t (g i) -> p g t i", i=4)
+        def weave(u, on_scalar):
+            width = pieces[units[u][0]][1]
+            woven[u] = keep.tile([P, width, PACK], BF16, name="woven%d" % u, tag="own%d" % u if on_scalar else "first%d" % (u + 1), align_bytes=64)
+            dst = woven[u][:].rearrange("p (g i) t -> p g t i", i=4)
+            src = signed[u][:].rearrange("p t (g i) -> p g t i", i=4)
             if on_scalar:
                 nc.scalar.copy(out=dst, in_=src)
             else:
                 nc.vector.tensor_copy(out=dst, in_=src)
 
-        def quantise(j0, width, a):
-            codes = ring.tile([P, width], U32, name="h_codes", bufs=3, align_bytes=64)
-            scales = ring.tile([P, width], U8, name="h_scales", bufs=3, align_bytes=64)
-            hq[(j0, a)] = (codes, scales)
-            nc.vector.quantize_mx(out=codes[:].bitcast(FP8X4), scales=scales[:], in_=woven[(j0, a)][:].rearrange("p j t -> p (j t)"))
+        def quantise(u):
+            width = pieces[units[u][0]][1]
+            codes = keep.tile([P, width], U32, name="h_codes%d" % u, tag="second%d" % (u + 1), align_bytes=64)
+            scales = keep.tile([P, width], U8, name="h_scales%d" % u, align_bytes=64)
+            hq[units[u]] = (codes, scales)
+            nc.vector.quantize_mx(out=codes[:].bitcast(FP8X4), scales=scales[:], in_=woven[u][:].rearrange("p j t -> p (j t)"))
 
-        def stage2(j0, width):
+        def stage2(k):
+            j0, width = pieces[k]
             run = CH if width == CH else P
             for nt in range(NT):
-                ybank = psum.tile([P, width], F32, name="ybank", bufs=2)
+                ybank = next_bank(width)
                 for a in range(HALVES):
-                    codes, scales = hq[(j0, a)]
+                    codes, scales = hq[(k, a)]
                     for s in range(0, width, run):
                         nc.tensor.matmul_mx(
                             out=ybank[:, s : s + run],
@@ -201,45 +237,38 @@ def tile_list_kg_sqd_bias_kernel(
                             start=(a == 0 and s == 0),
                             stop=(a == HALVES - 1 and s + run == width),
                         )
-                y = ring.tile([P, width], F32, name="y", bufs=4)
-                if j0 + width == J and nt == NT - 1:
-                    nc.vector.tensor_scalar(y[:], ybank[:], b_t[:, nt : nt + 1], None, ALU.add)
+                y = ring.tile([P, width], F32, name="y", bufs=6)
+                if k == len(pieces) - 1 and nt == NT - 1:
+                    nc.vector.tensor_scalar(y[:], ybank, b_t[:, nt : nt + 1], None, ALU.add)
                 else:
-                    nc.scalar.activation(out=y[:], in_=ybank[:], func=ACT.Identity, bias=b_t[:, nt : nt + 1])
+                    nc.scalar.activation(out=y[:], in_=ybank, func=ACT.Identity, bias=b_t[:, nt : nt + 1])
                 nc.sync.dma_start(out=out[nt * P : (nt + 1) * P, j0 : j0 + width], in_=y[:])
 
-        for c in range(3):
-            gather("s1", c)
-        for c in range(3):
-            gather("s2", c)
-        prepare_wb()
+        gather("s1", 0, NCH - 1)
+        gather("s2", 0, NCH - 1)
+        deal_wb_words(0)
+        deal_wb_scales()
         prepare_wa(0)
-        gather("w1", 0)
-        gather("w1", 1)
-        gather("w2", 0)
-        gather("w2", 1)
-        prepare_wa(1)
+        gather("w1", 0, 1)
+        gather("w2", 0, 1)
+        deal_wb_words(1)
+        gather("w1", 1, NCH - 1)
+        gather("w2", 1, NCH - 1)
 
-        pieces = [(0, CH), (CH, CH), (2 * CH, CH), (3 * CH, CH // 2), (3 * CH + CH // 2, CH // 2)]
-        units = [(j0, width, a) for (j0, width) in pieces for a in range(HALVES)]
-        SCALAR_WEAVES = (1, 3)
+        SCALAR_WEAVES = (0,)
+        FIRST_STAGE2 = 8
         for u in range(len(units) + 2):
             if u < len(units):
-                stage1(*units[u])
-                signs(*units[u])
+                stage1(u)
+                signs(u)
+            if u == 0:
+                prepare_wa(1)
+                for kind in ("s1", "s2", "w1", "w2"):
+                    gather(kind, NCH - 1, NCH)
             if 1 <= u <= len(units):
-                weave(*units[u - 1], u - 1 in SCALAR_WEAVES)
-            if u < len(units):
-                j0, width, a = units[u]
-                c = j0 // CH
-                if a == 1 and c + 2 < NCH:
-                    gather("w1", c + 2)
-                    gather("w2", c + 2)
-                if a == 1 and c + 3 < NCH:
-                    gather("s1", c + 3)
-                    gather("s2", c + 3)
+                weave(u - 1, u - 1 in SCALAR_WEAVES)
             if u >= 2:
-                j0, width, a = units[u - 2]
-                quantise(j0, width, a)
-                if a == 1:
-                    stage2(j0, width)
+                quantise(u - 2)
+            if u >= FIRST_STAGE2:
+                stage2(u - FIRST_STAGE2)
+        stage2(len(pieces) - 1)

@@ -24,6 +24,8 @@ CH = 512
 NCH = J // CH
 LISTCOLS = CH // 16
 NT = N // P
+TAB2_ROW = 4
+WB_ROW = 8
 
 
 def tile_list_kg_sqd_bias_kernel(
@@ -49,11 +51,10 @@ def tile_list_kg_sqd_bias_kernel(
         at_en = at_wb + 4 * KP
         at_b = at_en + HALVES * 2 * N
         at_sm = at_b + 64
-        at_mid = at_sm + 64
-        at_last = at_mid + 8 * CH
-        zeros = loads.tile([P, at_last // 4], I32, name="zeros", offset=0)
-        nc.vector.memset(tabs[:].bitcast(I32), 0)
-        nc.gpsimd.memset(tab2s[:].bitcast(I32), 0)
+        at_late = at_sm + 64 + 7 * CH
+        zeros = loads.tile([P, at_late // 4 + KP], I32, name="zeros", offset=0)
+        nc.gpsimd.memset(tabs[:].bitcast(I32), 0)
+        nc.vector.memset(tab2s[:].bitcast(I32), 0)
         nc.vector.memset(zeros[:, 0:1], 0)
         nc.vector.tensor_copy(out=wbs_raw[:].bitcast(I32), in_=zeros[:, 0:1].to_broadcast([P, R // 4]))
         nc.gpsimd.memset(ens[:].rearrange("p a n -> p (a n)").bitcast(I32), 0)
@@ -63,7 +64,7 @@ def tile_list_kg_sqd_bias_kernel(
         tabw = loads.tile([P, T], U32, name="tabw", align_bytes=64, offset=0)
         tab2w = loads.tile([P, T], U32, name="tab2w", align_bytes=64, offset=4 * T)
         wa_raw = [loads.tile([P, PACK, KP], F32, name="wa_raw%d" % a, offset=at_wa + HALF_BYTES * a) for a in range(HALVES)]
-        wb_raw = [loads.tile([P, KP], I32, name="wb_raw%d" % a, offset=(at_wb, at_mid)[a]) for a in range(HALVES)]
+        wb_raw = [loads.tile([P, KP], I32, name="wb_raw%d" % a, offset=(at_wb, at_late)[a]) for a in range(HALVES)]
         enw = loads.tile([P, HALVES, 2 * N], U8, name="enw", align_bytes=64, offset=at_en)
         b_t = loads.tile([P, NT], F32, name="b_t", offset=at_b)
         sm_t = loads.tile([P, HALVES, PACK], F32, name="sm_t", offset=at_sm)
@@ -75,10 +76,10 @@ def tile_list_kg_sqd_bias_kernel(
         nc.sync.dma_start(out=wa_raw[0][:], in_=wa_rows[:, :, 0:KP])
         nc.sync.dma_start(out=sm_t[:], in_=sm.rearrange("(a p t) -> p a t", a=HALVES, t=PACK))
         for q in range(4):
-            nc.sync.dma_start(out=tab2s[32 * q : 32 * q + 4, :].bitcast(I32), in_=tab2_scales[0, 4 * q : 4 * q + 4, :].bitcast(I32))
+            nc.sync.dma_start(out=tab2s[32 * q + TAB2_ROW : 32 * q + TAB2_ROW + 4, :].bitcast(I32), in_=tab2_scales[0, 4 * q : 4 * q + 4, :].bitcast(I32))
         nc.sync.dma_start(out=wb_raw[0][:], in_=wb_flat[:, 0:KP])
         for q in range(4):
-            nc.sync.dma_start(out=wbs_raw[32 * q : 32 * q + 4, :].bitcast(I32), in_=wb_scales[0, 4 * q : 4 * q + 4, :].bitcast(I32))
+            nc.sync.dma_start(out=wbs_raw[32 * q + WB_ROW : 32 * q + WB_ROW + 4, :].bitcast(I32), in_=wb_scales[0, 4 * q : 4 * q + 4, :].bitcast(I32))
         nc.sync.dma_start(out=tabw[:].bitcast(I32), in_=tab_words[0].rearrange("p t i -> p (t i)").bitcast(I32))
         nc.sync.dma_start(out=tab2w[:].bitcast(I32), in_=tab2_words[0].rearrange("p t i -> p (t i)").bitcast(I32))
         nc.sync.dma_start(out=wb_raw[1][:], in_=wb_flat[:, KP:R])
@@ -139,7 +140,7 @@ def tile_list_kg_sqd_bias_kernel(
             )
 
         picked = {}
-        last_at = {"w1": at_last, "s1": at_last + 4 * CH, "s2": at_last + 5 * CH, "w2": at_last + 6 * CH}
+        late_at = {("w1", 1): at_late - 7 * CH, ("s1", 3): at_late + CH, ("s2", 3): at_late + 2 * CH, ("w1", 3): at_late + 3 * CH}
 
         def gather(kind, c0, c1):
             table, offsets, dtype = {
@@ -150,10 +151,8 @@ def tile_list_kg_sqd_bias_kernel(
             }[kind]
             name = "picked_%s_%d" % (kind, c0)
             shape = [P, (c1 - c0) * CH]
-            if c0 == NCH - 1:
-                dst = loads.tile(shape, dtype, name=name, align_bytes=64, offset=last_at[kind])
-            elif kind == "w1" and c0 > 0:
-                dst = loads.tile(shape, dtype, name=name, align_bytes=64, offset=at_mid)
+            if (kind, c0) in late_at:
+                dst = loads.tile(shape, dtype, name=name, align_bytes=64, offset=late_at[(kind, c0)])
             else:
                 dst = keep.tile(shape, dtype, name=name, align_bytes=64)
             nc.vector.tensor_copy(dst[:], table[:].indirect(offsets[:, c0 * LISTCOLS : c1 * LISTCOLS]))
@@ -167,21 +166,20 @@ def tile_list_kg_sqd_bias_kernel(
             turn.append(width)
             return banks[(len(turn) - 1) % 8][:, 0:width]
 
-        pieces = [(0, CH), (CH, CH), (2 * CH, CH), (3 * CH, CH // 2), (3 * CH + CH // 2, CH // 2)]
-        units = [(0, 0), (1, 0), (0, 1), (1, 1)] + [(k, a) for k in range(2, len(pieces)) for a in range(HALVES)]
+        H = CH // 2
+        units = [(0, 2 * CH, 0), (2 * CH, 2 * CH, 0), (0, 2 * CH, 1), (2 * CH, CH, 1), (3 * CH, H, 1), (3 * CH + H, H, 1)]
+        pieces = [(0, CH), (CH, CH), (2 * CH, CH), (3 * CH, H), (3 * CH + H, H)]
         squares, signed, woven, hq = {}, {}, {}, {}
 
-        def stage1(u):
-            k, a = units[u]
-            j0, width = pieces[k]
-            c = j0 // CH
-            js = slice(j0 - c * CH, j0 - c * CH + width)
-            if u == 0:
-                squares[u] = loads.tile([P, PACK, width], BF16, name="squares0", align_bytes=64, offset=at_last + 3 * CH)
-            else:
-                squares[u] = keep.tile([P, PACK, width], BF16, name="squares%d" % u, tag="first%d" % u, align_bytes=64)
+        def stage1(u, part):
+            j0, width, a = units[u]
+            if part == 0:
+                squares[u] = keep.tile([P, PACK, width], BF16, name="squares%d" % u, align_bytes=64)
+            run = min(width, CH)
+            c, start = divmod(j0 + part * run, CH)
+            js = slice(start, start + run)
             for t in range(PACK):
-                bank = next_bank(width)
+                bank = next_bank(run)
                 cols = slice(t * P, (t + 1) * P)
                 scols = slice(a * KP + t * P, a * KP + (t + 1) * P)
                 nc.tensor.matmul_mx(
@@ -189,36 +187,34 @@ def tile_list_kg_sqd_bias_kernel(
                     rhs=picked[("w1", c)][:, js].bitcast(FP8X4), rhs_scale=picked[("s1", c)][:, js], start=True, stop=False,
                 )
                 nc.tensor.matmul_mx(
-                    out=bank, lhsT=wb_codes[a][:, cols].bitcast(FP8X4), lhsT_scale=wbs[:, scols],
-                    rhs=picked[("w2", c)][:, js].bitcast(FP8X4), rhs_scale=picked[("s2", c)][:, js], start=False, stop=True,
+                    out=bank, lhsT=wb_codes[a][:, cols].bitcast(FP8X4), lhsT_scale=wbs[WB_ROW:P, scols],
+                    rhs=picked[("w2", c)][:, js].bitcast(FP8X4), rhs_scale=picked[("s2", c)][TAB2_ROW:P, js], start=False, stop=True,
                 )
                 col = a * PACK + t
-                nc.scalar.activation(out=squares[u][:, t, :], in_=bank, func=ACT.Square, scale=root[:, col : col + 1])
+                nc.scalar.activation(out=squares[u][:, t, part * run : (part + 1) * run], in_=bank, func=ACT.Square, scale=root[:, col : col + 1])
 
         def signs(u):
-            k, a = units[u]
-            width = pieces[k][1]
-            signed[u] = keep.tile([P, PACK, width], BF16, name="signed%d" % u, tag="second%d" % u, align_bytes=64)
+            j0, width, a = units[u]
+            signed[u] = keep.tile([P, PACK, width], BF16, name="signed%d" % u, align_bytes=64)
             for t in range(PACK):
                 col = a * PACK + t
                 nc.vector.tensor_scalar(signed[u][:, t, :], squares[u][:, t, :], sgn[:, col : col + 1], None, ALU.mult)
 
-        def weave(u, on_scalar):
-            width = pieces[units[u][0]][1]
-            woven[u] = keep.tile([P, width, PACK], BF16, name="woven%d" % u, tag="own%d" % u if on_scalar else "first%d" % (u + 1), align_bytes=64)
-            dst = woven[u][:].rearrange("p (g i) t -> p g t i", i=4)
-            src = signed[u][:].rearrange("p t (g i) -> p g t i", i=4)
-            if on_scalar:
-                nc.scalar.copy(out=dst, in_=src)
-            else:
-                nc.vector.tensor_copy(out=dst, in_=src)
+        def weave(u):
+            width = units[u][1]
+            woven[u] = keep.tile([P, width, PACK], BF16, name="woven%d" % u, align_bytes=64)
+            nc.vector.tensor_copy(
+                out=woven[u][:].rearrange("p (g i) t -> p g t i", i=4),
+                in_=signed[u][:].rearrange("p t (g i) -> p g t i", i=4),
+            )
 
         def quantise(u):
-            width = pieces[units[u][0]][1]
-            codes = keep.tile([P, width], U32, name="h_codes%d" % u, tag="second%d" % (u + 1), align_bytes=64)
+            j0, width, a = units[u]
+            codes = keep.tile([P, width], U32, name="h_codes%d" % u, align_bytes=64)
             scales = keep.tile([P, width], U8, name="h_scales%d" % u, align_bytes=64)
-            hq[units[u]] = (codes, scales)
             nc.vector.quantize_mx(out=codes[:].bitcast(FP8X4), scales=scales[:], in_=woven[u][:].rearrange("p j t -> p (j t)"))
+            for s in range(0, width, P):
+                hq[(j0 + s, a)] = (codes, scales, s)
 
         def stage2(k):
             j0, width = pieces[k]
@@ -226,14 +222,14 @@ def tile_list_kg_sqd_bias_kernel(
             for nt in range(NT):
                 ybank = next_bank(width)
                 for a in range(HALVES):
-                    codes, scales = hq[(k, a)]
                     for s in range(0, width, run):
+                        codes, scales, at = hq[(j0 + s, a)]
                         nc.tensor.matmul_mx(
                             out=ybank[:, s : s + run],
                             lhsT=enw[:, a, 2 * nt * P : 2 * (nt + 1) * P].bitcast(FP4X4),
                             lhsT_scale=ens[:, a, nt * P : (nt + 1) * P],
-                            rhs=codes[:, s : s + run].bitcast(FP8X4),
-                            rhs_scale=scales[:, s : s + run],
+                            rhs=codes[:, at : at + run].bitcast(FP8X4),
+                            rhs_scale=scales[:, at : at + run],
                             start=(a == 0 and s == 0),
                             stop=(a == HALVES - 1 and s + run == width),
                         )
@@ -255,20 +251,16 @@ def tile_list_kg_sqd_bias_kernel(
         gather("w1", 1, NCH - 1)
         gather("w2", 1, NCH - 1)
 
-        SCALAR_WEAVES = (0,)
-        FIRST_STAGE2 = 8
-        for u in range(len(units) + 2):
-            if u < len(units):
-                stage1(u)
-                signs(u)
-            if u == 0:
-                prepare_wa(1)
-                for kind in ("s1", "s2", "w1", "w2"):
-                    gather(kind, NCH - 1, NCH)
-            if 1 <= u <= len(units):
-                weave(u - 1, u - 1 in SCALAR_WEAVES)
-            if u >= 2:
-                quantise(u - 2)
-            if u >= FIRST_STAGE2:
-                stage2(u - FIRST_STAGE2)
-        stage2(len(pieces) - 1)
+        for kind in ("s1", "s2", "w1", "w2"):
+            gather(kind, NCH - 1, NCH)
+
+        for u in range(len(units)):
+            for part in range(max(1, units[u][1] // CH)):
+                stage1(u, part)
+                if u == 0 and part == 0:
+                    prepare_wa(1)
+            signs(u)
+            weave(u)
+            quantise(u)
+        for k in range(len(pieces)):
+            stage2(k)

@@ -128,19 +128,26 @@ def tile_list_kg_sqd_bias_kernel(
             nc.vector.quantize_mx(out=wa_codes[a][:].bitcast(FP8X4), scales=wa_scales[a][:], in_=wa_bf[:].rearrange("p t m i -> p (t m i)"))
 
         def deal_wb_words(a):
-            nc.vector.tensor_copy(
-                out=wb_codes[a][:].rearrange("p (t m) -> p m t", t=PACK),
-                in_=wb_raw[a][:].rearrange("p (m t) -> p m t", t=PACK),
-            )
+            if a == 0:
+                nc.gpsimd.tensor_copy(
+                    out=wb_codes[a][:].rearrange("p (t m) -> p t m", t=PACK),
+                    in_=wb_raw[a][:].rearrange("p (m t) -> p t m", t=PACK),
+                )
+            else:
+                nc.vector.tensor_copy(
+                    out=wb_codes[a][:].rearrange("p (t m) -> p m t", t=PACK),
+                    in_=wb_raw[a][:].rearrange("p (m t) -> p m t", t=PACK),
+                )
 
         def deal_wb_scales():
-            nc.vector.tensor_copy(
-                out=wbs[:].rearrange("p (a t m) -> p a m t", a=HALVES, t=PACK),
-                in_=wbs_raw[:].rearrange("p (a m t) -> p a m t", a=HALVES, t=PACK),
-            )
+            for a in range(HALVES):
+                nc.gpsimd.tensor_copy(
+                    out=wbs[:, a * KP : (a + 1) * KP].rearrange("p (t m) -> p t m", t=PACK),
+                    in_=wbs_raw[:, a * KP : (a + 1) * KP].rearrange("p (m t) -> p t m", t=PACK),
+                )
 
         picked = {}
-        late_at = {("w1", 1): at_late - 7 * CH, ("s1", 3): at_late + CH, ("s2", 3): at_late + 2 * CH, ("w1", 3): at_late + 3 * CH}
+        late_at = {("w1", 1): at_late - 7 * CH, ("w1", 3): at_late + 3 * CH}
 
         def gather(kind, c0, c1):
             table, offsets, dtype = {
@@ -167,35 +174,35 @@ def tile_list_kg_sqd_bias_kernel(
             return banks[(len(turn) - 1) % 8][:, 0:width]
 
         H = CH // 2
-        units = [(0, 2 * CH, 0), (2 * CH, 2 * CH, 0), (0, 2 * CH, 1), (2 * CH, CH, 1), (3 * CH, H, 1), (3 * CH + H, H, 1)]
+        units = [(0, CH, 0), (CH, CH, 0), (2 * CH, 2 * CH, 0), (0, 2 * CH, 1), (2 * CH, CH, 1), (3 * CH, H, 1), (3 * CH + H, H, 1)]
         pieces = [(0, CH), (CH, CH), (2 * CH, CH), (3 * CH, H), (3 * CH + H, H)]
         squares, signed, woven, hq = {}, {}, {}, {}
 
-        def stage1(u, part):
+        def stage1(u):
             j0, width, a = units[u]
-            if part == 0:
-                squares[u] = keep.tile([P, PACK, width], BF16, name="squares%d" % u, align_bytes=64)
+            squares[u] = keep.tile([P, PACK, width], BF16, name="squares%d" % u, align_bytes=64)
             run = min(width, CH)
-            c, start = divmod(j0 + part * run, CH)
-            js = slice(start, start + run)
             for t in range(PACK):
-                bank = next_bank(run)
                 cols = slice(t * P, (t + 1) * P)
                 scols = slice(a * KP + t * P, a * KP + (t + 1) * P)
-                nc.tensor.matmul_mx(
-                    out=bank, lhsT=wa_codes[a][:, cols].bitcast(FP8X4), lhsT_scale=wa_scales[a][:, cols],
-                    rhs=picked[("w1", c)][:, js].bitcast(FP8X4), rhs_scale=picked[("s1", c)][:, js], start=True, stop=False,
-                )
-                nc.tensor.matmul_mx(
-                    out=bank, lhsT=wb_codes[a][:, cols].bitcast(FP8X4), lhsT_scale=wbs[WB_ROW:P, scols],
-                    rhs=picked[("w2", c)][:, js].bitcast(FP8X4), rhs_scale=picked[("s2", c)][TAB2_ROW:P, js], start=False, stop=True,
-                )
                 col = a * PACK + t
-                nc.scalar.activation(out=squares[u][:, t, part * run : (part + 1) * run], in_=bank, func=ACT.Square, scale=root[:, col : col + 1])
+                for s in range(0, width, run):
+                    c, start = divmod(j0 + s, CH)
+                    js = slice(start, start + run)
+                    bank = next_bank(run)
+                    nc.tensor.matmul_mx(
+                        out=bank, lhsT=wa_codes[a][:, cols].bitcast(FP8X4), lhsT_scale=wa_scales[a][:, cols],
+                        rhs=picked[("w1", c)][:, js].bitcast(FP8X4), rhs_scale=picked[("s1", c)][:, js], start=True, stop=False,
+                    )
+                    nc.tensor.matmul_mx(
+                        out=bank, lhsT=wb_codes[a][:, cols].bitcast(FP8X4), lhsT_scale=wbs[WB_ROW:P, scols],
+                        rhs=picked[("w2", c)][:, js].bitcast(FP8X4), rhs_scale=picked[("s2", c)][TAB2_ROW:P, js], start=False, stop=True,
+                    )
+                    nc.scalar.activation(out=squares[u][:, t, s : s + run], in_=bank, func=ACT.Square, scale=root[:, col : col + 1])
 
         def signs(u):
             j0, width, a = units[u]
-            signed[u] = keep.tile([P, PACK, width], BF16, name="signed%d" % u, align_bytes=64)
+            signed[u] = keep.tile([P, PACK, width], BF16, name="signed%d" % u, tag="signed%d" % u, align_bytes=64)
             for t in range(PACK):
                 col = a * PACK + t
                 nc.vector.tensor_scalar(signed[u][:, t, :], squares[u][:, t, :], sgn[:, col : col + 1], None, ALU.mult)
@@ -208,9 +215,20 @@ def tile_list_kg_sqd_bias_kernel(
                 in_=signed[u][:].rearrange("p t (g i) -> p g t i", i=4),
             )
 
+        def sign_and_weave_on_gpsimd(u):
+            j0, width, a = units[u]
+            woven[u] = keep.tile([P, width, PACK], BF16, name="woven%d" % u, align_bytes=64)
+            for s in range(0, width, P):
+                nc.gpsimd.tensor_tensor(
+                    woven[u][:, s : s + P, :],
+                    squares[u][:, :, s : s + P].rearrange("p t j -> p j t"),
+                    sgn[:, a * PACK : (a + 1) * PACK].unsqueeze(1).to_broadcast([P, P, PACK]),
+                    ALU.mult,
+                )
+
         def quantise(u):
             j0, width, a = units[u]
-            codes = keep.tile([P, width], U32, name="h_codes%d" % u, align_bytes=64)
+            codes = keep.tile([P, width], U32, name="h_codes%d" % u, tag="signed1" if u == 0 else "codes%d" % u, align_bytes=64)
             scales = keep.tile([P, width], U8, name="h_scales%d" % u, align_bytes=64)
             nc.vector.quantize_mx(out=codes[:].bitcast(FP8X4), scales=scales[:], in_=woven[u][:].rearrange("p j t -> p (j t)"))
             for s in range(0, width, P):
@@ -234,14 +252,14 @@ def tile_list_kg_sqd_bias_kernel(
                             stop=(a == HALVES - 1 and s + run == width),
                         )
                 y = ring.tile([P, width], F32, name="y", bufs=6)
-                if k == len(pieces) - 1 and nt == NT - 1:
+                if k >= 3 and nt == NT - 1:
                     nc.vector.tensor_scalar(y[:], ybank, b_t[:, nt : nt + 1], None, ALU.add)
                 else:
                     nc.scalar.activation(out=y[:], in_=ybank, func=ACT.Identity, bias=b_t[:, nt : nt + 1])
                 nc.sync.dma_start(out=out[nt * P : (nt + 1) * P, j0 : j0 + width], in_=y[:])
 
-        gather("s1", 0, NCH - 1)
-        gather("s2", 0, NCH - 1)
+        gather("s1", 0, NCH)
+        gather("s2", 0, NCH)
         deal_wb_words(0)
         deal_wb_scales()
         prepare_wa(0)
@@ -251,16 +269,19 @@ def tile_list_kg_sqd_bias_kernel(
         gather("w1", 1, NCH - 1)
         gather("w2", 1, NCH - 1)
 
-        for kind in ("s1", "s2", "w1", "w2"):
+        for kind in ("w1", "w2"):
             gather(kind, NCH - 1, NCH)
 
         for u in range(len(units)):
-            for part in range(max(1, units[u][1] // CH)):
-                stage1(u, part)
-                if u == 0 and part == 0:
-                    prepare_wa(1)
-            signs(u)
-            weave(u)
-            quantise(u)
+            stage1(u)
+            if u == 0:
+                prepare_wa(1)
+                sign_and_weave_on_gpsimd(u)
+            else:
+                signs(u)
+                weave(u)
+                if u == 1:
+                    quantise(0)
+                quantise(u)
         for k in range(len(pieces)):
             stage2(k)

@@ -18,14 +18,18 @@ ALU = mybir.AluOpType
 
 P = 128
 PACK = 4
-KP = P * PACK
-HALVES = R // KP
-CH = 512
-NCH = J // CH
-LISTCOLS = CH // 16
-NT = N // P
+PASS = P * PACK
+HALVES = R // PASS
+CHUNK = 512
+LIST_COLS = CHUNK // 16
+N_TILES = N // P
+QUADRANTS = 4
+BANKS = 8
 TAB2_ROW = 4
 WB_ROW = 8
+GPSIMD_COLUMNS = 256
+VECTOR_FROM_PIECE = 2
+OUT_BUFS = 6
 
 
 def tile_list_kg_sqd_bias_kernel(
@@ -35,253 +39,250 @@ def tile_list_kg_sqd_bias_kernel(
     with ExitStack() as ctx:
         lists = ctx.enter_context(tc.tile_pool(name="lists", bufs=1))
         keep = ctx.enter_context(tc.tile_pool(name="keep", bufs=1))
-        loads = ctx.enter_context(tc.tile_pool(name="loads", bufs=1))
-        ring = ctx.enter_context(tc.tile_pool(name="ring", bufs=2))
+        placed = ctx.enter_context(tc.tile_pool(name="placed", bufs=1))
+        ring = ctx.enter_context(tc.tile_pool(name="ring", bufs=OUT_BUFS))
         psum = ctx.enter_context(tc.psum_pool(name="psum", bufs=1))
 
         offs_t = lists.tile([P, J // 16], U16, name="offs_t")
         offs2_t = lists.tile([P, J // 16], U16, name="offs2_t")
-        tabs = keep.tile([P, T], U8, name="tabs", align_bytes=64)
-        tab2s = keep.tile([P, T], U8, name="tab2s", align_bytes=64)
-        wbs_raw = keep.tile([P, R], U8, name="wbs_raw", align_bytes=64)
-        ens = keep.tile([P, HALVES, N], U8, name="ens", align_bytes=64)
-        HALF_BYTES = 4 * PACK * KP
-        at_wa = 8 * T
-        at_wb = at_wa + HALVES * HALF_BYTES
-        at_en = at_wb + 4 * KP
+        tab_s = keep.tile([P, T], U8, name="tab_s", align_bytes=64)
+        tab2_s = keep.tile([P, T], U8, name="tab2_s", align_bytes=64)
+        wb_s_raw = keep.tile([P, R], U8, name="wb_s_raw", align_bytes=64)
+        en_s = keep.tile([P, HALVES, N], U8, name="en_s", align_bytes=64)
+
+        word_bytes = 4
+        wa_half_bytes = word_bytes * PACK * PASS
+        at_tab2 = word_bytes * T
+        at_wa = 2 * word_bytes * T
+        at_wb0 = at_wa + HALVES * wa_half_bytes
+        at_en = at_wb0 + word_bytes * PASS
         at_b = at_en + HALVES * 2 * N
         at_sm = at_b + 64
-        at_late = at_sm + 64 + 7 * CH
-        zeros = loads.tile([P, at_late // 4 + KP], I32, name="zeros", offset=0)
-        nc.gpsimd.memset(tabs[:].bitcast(I32), 0)
-        nc.vector.memset(tab2s[:].bitcast(I32), 0)
+        at_w1_late = at_sm + 64
+        at_s2_late = at_w1_late + word_bytes * 2 * CHUNK
+        at_wb1 = at_s2_late - CHUNK
+
+        zeros = placed.tile([P, at_wb1 // word_bytes + PASS], I32, name="zeros", offset=0)
+        nc.gpsimd.memset(tab_s[:].bitcast(I32), 0)
+        nc.vector.memset(tab2_s[:].bitcast(I32), 0)
         nc.vector.memset(zeros[:, 0:1], 0)
-        nc.vector.tensor_copy(out=wbs_raw[:].bitcast(I32), in_=zeros[:, 0:1].to_broadcast([P, R // 4]))
-        nc.gpsimd.memset(ens[:].rearrange("p a n -> p (a n)").bitcast(I32), 0)
+        nc.vector.tensor_copy(out=wb_s_raw[:].bitcast(I32), in_=zeros[:, 0:1].to_broadcast([P, R // word_bytes]))
+        nc.gpsimd.memset(en_s[:].rearrange("p a n -> p (a n)").bitcast(I32), 0)
 
         wa_rows = wa.rearrange("(p i) r -> p i r", i=PACK)
         wb_flat = wb_words[0].rearrange("p r i -> p (r i)").bitcast(I32)
-        tabw = loads.tile([P, T], U32, name="tabw", align_bytes=64, offset=0)
-        tab2w = loads.tile([P, T], U32, name="tab2w", align_bytes=64, offset=4 * T)
-        wa_raw = [loads.tile([P, PACK, KP], F32, name="wa_raw%d" % a, offset=at_wa + HALF_BYTES * a) for a in range(HALVES)]
-        wb_raw = [loads.tile([P, KP], I32, name="wb_raw%d" % a, offset=(at_wb, at_late)[a]) for a in range(HALVES)]
-        enw = loads.tile([P, HALVES, 2 * N], U8, name="enw", align_bytes=64, offset=at_en)
-        b_t = loads.tile([P, NT], F32, name="b_t", offset=at_b)
-        sm_t = loads.tile([P, HALVES, PACK], F32, name="sm_t", offset=at_sm)
+        tab_w = placed.tile([P, T], U32, name="tab_w", align_bytes=64, offset=0)
+        tab2_w = placed.tile([P, T], U32, name="tab2_w", align_bytes=64, offset=at_tab2)
+        wa_raw = [placed.tile([P, PACK, PASS], F32, name="wa_raw%d" % a, offset=at_wa + wa_half_bytes * a) for a in range(HALVES)]
+        wb_raw = [placed.tile([P, PASS], I32, name="wb_raw%d" % a, offset=(at_wb0, at_wb1)[a]) for a in range(HALVES)]
+        en_w = placed.tile([P, HALVES, 2 * N], U8, name="en_w", align_bytes=64, offset=at_en)
+        b_t = placed.tile([P, N_TILES], F32, name="b_t", offset=at_b)
+        sm_t = placed.tile([P, HALVES, PACK], F32, name="sm_t", offset=at_sm)
+
+        def load_scale_rows(dst, first, rows):
+            for q in range(QUADRANTS):
+                nc.sync.dma_start(out=dst[32 * q + first : 32 * q + first + 4, :].bitcast(I32), in_=rows[4 * q : 4 * q + 4, :].bitcast(I32))
 
         nc.sync.dma_start(offs_t[:], offs)
-        for q in range(4):
-            nc.sync.dma_start(out=tabs[32 * q : 32 * q + 4, :].bitcast(I32), in_=tab_scales[0, 4 * q : 4 * q + 4, :].bitcast(I32))
+        load_scale_rows(tab_s, 0, tab_scales[0])
         nc.sync.dma_start(offs2_t[:], offs2)
-        nc.sync.dma_start(out=wa_raw[0][:], in_=wa_rows[:, :, 0:KP])
+        nc.sync.dma_start(out=wa_raw[0][:], in_=wa_rows[:, :, 0:PASS])
         nc.sync.dma_start(out=sm_t[:], in_=sm.rearrange("(a p t) -> p a t", a=HALVES, t=PACK))
-        for q in range(4):
-            nc.sync.dma_start(out=tab2s[32 * q + TAB2_ROW : 32 * q + TAB2_ROW + 4, :].bitcast(I32), in_=tab2_scales[0, 4 * q : 4 * q + 4, :].bitcast(I32))
-        nc.sync.dma_start(out=wb_raw[0][:], in_=wb_flat[:, 0:KP])
-        for q in range(4):
-            nc.sync.dma_start(out=wbs_raw[32 * q + WB_ROW : 32 * q + WB_ROW + 4, :].bitcast(I32), in_=wb_scales[0, 4 * q : 4 * q + 4, :].bitcast(I32))
-        nc.sync.dma_start(out=tabw[:].bitcast(I32), in_=tab_words[0].rearrange("p t i -> p (t i)").bitcast(I32))
-        nc.sync.dma_start(out=tab2w[:].bitcast(I32), in_=tab2_words[0].rearrange("p t i -> p (t i)").bitcast(I32))
-        nc.sync.dma_start(out=wb_raw[1][:], in_=wb_flat[:, KP:R])
-        nc.sync.dma_start(out=wa_raw[1][:], in_=wa_rows[:, :, KP:R])
-        nc.sync.dma_start(out=enw[:].bitcast(I32), in_=en_words.rearrange("a p n -> p a n").bitcast(I32))
-        for q in range(4):
+        load_scale_rows(tab2_s, TAB2_ROW, tab2_scales[0])
+        nc.sync.dma_start(out=wb_raw[0][:], in_=wb_flat[:, 0:PASS])
+        load_scale_rows(wb_s_raw, WB_ROW, wb_scales[0])
+        nc.sync.dma_start(out=tab_w[:].bitcast(I32), in_=tab_words[0].rearrange("p t i -> p (t i)").bitcast(I32))
+        nc.sync.dma_start(out=tab2_w[:].bitcast(I32), in_=tab2_words[0].rearrange("p t i -> p (t i)").bitcast(I32))
+        nc.sync.dma_start(out=wb_raw[1][:], in_=wb_flat[:, PASS:R])
+        nc.sync.dma_start(out=wa_raw[1][:], in_=wa_rows[:, :, PASS:R])
+        nc.sync.dma_start(out=en_w[:].bitcast(I32), in_=en_words.rearrange("a p n -> p a n").bitcast(I32))
+        for q in range(QUADRANTS):
             nc.sync.dma_start(
-                out=ens[32 * q : 32 * q + 4, :, :].bitcast(I32),
+                out=en_s[32 * q : 32 * q + 4, :, :].bitcast(I32),
                 in_=en_scales[:, 4 * q : 4 * q + 4, :].rearrange("a q n -> q a n").bitcast(I32),
             )
         with nc.allow_non_contiguous_dma(reason="one bias value a partition"):
             nc.sync.dma_start(out=b_t[:], in_=b.rearrange("(c p) -> p c", p=P))
 
-        W = HALVES * PACK
-        smf = sm_t[:].rearrange("p a t -> p (a t)")
-        sgn = keep.tile([P, W], F32, name="sgn")
-        mag = keep.tile([P, W], F32, name="mag")
-        guess = keep.tile([P, W], F32, name="guess")
-        guess_sq = keep.tile([P, W], F32, name="guess_sq")
-        half_inv = keep.tile([P, W], F32, name="half_inv")
-        resid = keep.tile([P, W], F32, name="resid")
-        root = keep.tile([P, W], F32, name="root")
-        nc.scalar.activation(out=half_inv[:], in_=smf, func=ACT.Abs_reciprocal_sqrt, scale=4.0)
-        nc.scalar.activation(out=mag[:], in_=smf, func=ACT.Abs)
+        factors = HALVES * PACK
+        sm_flat = sm_t[:].rearrange("p a t -> p (a t)")
+        sgn = keep.tile([P, factors], F32, name="sgn")
+        mag = keep.tile([P, factors], F32, name="mag")
+        guess = keep.tile([P, factors], F32, name="guess")
+        guess_sq = keep.tile([P, factors], F32, name="guess_sq")
+        half_inv = keep.tile([P, factors], F32, name="half_inv")
+        resid = keep.tile([P, factors], F32, name="resid")
+        root = keep.tile([P, factors], F32, name="root")
+        nc.scalar.activation(out=half_inv[:], in_=sm_flat, func=ACT.Abs_reciprocal_sqrt, scale=4.0)
+        nc.scalar.activation(out=mag[:], in_=sm_flat, func=ACT.Abs)
         nc.scalar.activation(out=guess[:], in_=mag[:], func=ACT.Sqrt)
-        nc.scalar.activation(out=sgn[:], in_=smf, func=ACT.Sign)
+        nc.scalar.activation(out=sgn[:], in_=sm_flat, func=ACT.Sign)
         nc.scalar.activation(out=guess_sq[:], in_=guess[:], func=ACT.Square)
         nc.gpsimd.tensor_tensor(resid[:], mag[:], guess_sq[:], ALU.subtract)
         nc.gpsimd.tensor_scalar(half_inv[:], half_inv[:], 2.0**62, 1.0, ALU.min, ALU.mult)
         nc.gpsimd.tensor_tensor(resid[:], resid[:], half_inv[:], ALU.mult)
         nc.gpsimd.tensor_tensor(root[:], guess[:], resid[:], ALU.add)
 
-        wa_codes = [keep.tile([P, KP], U32, name="wa_codes%d" % a, align_bytes=64) for a in range(HALVES)]
-        wa_scales = [keep.tile([P, KP], U8, name="wa_scales%d" % a, align_bytes=64) for a in range(HALVES)]
-        wb_codes = [keep.tile([P, KP], I32, name="wb_codes%d" % a, align_bytes=64) for a in range(HALVES)]
-        wbs = keep.tile([P, R], U8, name="wbs", align_bytes=64)
+        wa_codes = [keep.tile([P, PASS], U32, name="wa_codes%d" % a, align_bytes=64) for a in range(HALVES)]
+        wa_s = [keep.tile([P, PASS], U8, name="wa_s%d" % a, align_bytes=64) for a in range(HALVES)]
+        wb_codes = [keep.tile([P, PASS], I32, name="wb_codes%d" % a, align_bytes=64) for a in range(HALVES)]
+        wb_s = keep.tile([P, R], U8, name="wb_s", align_bytes=64)
 
-        def prepare_wa(a):
+        def quantise_wa(a):
             wa_bf = keep.tile([P, PACK, P, PACK], BF16, name="wa_bf%d" % a, align_bytes=64)
-            nc.scalar.activation(
-                out=wa_bf[:].rearrange("p t m i -> p m i t"),
-                in_=wa_raw[a][:].rearrange("p i (m t) -> p m i t", t=PACK),
-                func=ACT.Copy,
-                scale=-1.0,
-            )
-            nc.vector.quantize_mx(out=wa_codes[a][:].bitcast(FP8X4), scales=wa_scales[a][:], in_=wa_bf[:].rearrange("p t m i -> p (t m i)"))
-
-        def deal_wb_words(a):
             if a == 0:
-                nc.gpsimd.tensor_copy(
-                    out=wb_codes[a][:].rearrange("p (t m) -> p t m", t=PACK),
-                    in_=wb_raw[a][:].rearrange("p (m t) -> p t m", t=PACK),
+                nc.scalar.activation(
+                    out=wa_bf[:].rearrange("p t m i -> p m i t"),
+                    in_=wa_raw[a][:].rearrange("p i (m t) -> p m i t", t=PACK),
+                    func=ACT.Copy,
+                    scale=-1.0,
                 )
             else:
-                nc.vector.tensor_copy(
-                    out=wb_codes[a][:].rearrange("p (t m) -> p m t", t=PACK),
-                    in_=wb_raw[a][:].rearrange("p (m t) -> p m t", t=PACK),
-                )
+                dealt = wa_raw[a][:].rearrange("p i (m t) -> p t m i", t=PACK)
+                for t in range(PACK):
+                    nc.gpsimd.tensor_scalar(wa_bf[:, t, :, :], dealt[:, t, :, :], -1.0, 0.0, ALU.mult, ALU.add)
+            nc.vector.quantize_mx(out=wa_codes[a][:].bitcast(FP8X4), scales=wa_s[a][:], in_=wa_bf[:].rearrange("p t m i -> p (t m i)"))
 
-        def deal_wb_scales():
-            for a in range(HALVES):
-                nc.gpsimd.tensor_copy(
-                    out=wbs[:, a * KP : (a + 1) * KP].rearrange("p (t m) -> p t m", t=PACK),
-                    in_=wbs_raw[:, a * KP : (a + 1) * KP].rearrange("p (m t) -> p t m", t=PACK),
-                )
+        def deal_columns(dst, src):
+            nc.gpsimd.tensor_copy(out=dst.rearrange("p (t m) -> p t m", t=PACK), in_=src.rearrange("p (m t) -> p t m", t=PACK))
 
         picked = {}
-        late_at = {("w1", 1): at_late - 7 * CH, ("w1", 3): at_late + 3 * CH}
 
-        def gather(kind, c0, c1):
-            table, offsets, dtype = {
-                "s1": (tabs, offs_t, U8),
-                "s2": (tab2s, offs2_t, U8),
-                "w1": (tabw, offs_t, U32),
-                "w2": (tab2w, offs2_t, U32),
-            }[kind]
-            name = "picked_%s_%d" % (kind, c0)
-            shape = [P, (c1 - c0) * CH]
-            if (kind, c0) in late_at:
-                dst = loads.tile(shape, dtype, name=name, align_bytes=64, offset=late_at[(kind, c0)])
-            else:
-                dst = keep.tile(shape, dtype, name=name, align_bytes=64)
-            nc.vector.tensor_copy(dst[:], table[:].indirect(offsets[:, c0 * LISTCOLS : c1 * LISTCOLS]))
+        def gather(kind, c0, c1, dst):
+            table, offsets = {"s1": (tab_s, offs_t), "s2": (tab2_s, offs2_t), "w1": (tab_w, offs_t), "w2": (tab2_w, offs2_t)}[kind]
+            nc.vector.tensor_copy(dst, table[:].indirect(offsets[:, c0 * LIST_COLS : c1 * LIST_COLS]))
             for c in range(c0, c1):
-                picked[(kind, c)] = dst[:, (c - c0) * CH : (c - c0 + 1) * CH]
+                picked[(kind, c)] = dst[:, (c - c0) * CHUNK : (c - c0 + 1) * CHUNK]
 
-        banks = [psum.tile([P, CH], F32, name="bank%d" % i) for i in range(8)]
-        turn = []
+        banks = [psum.tile([P, CHUNK], F32, name="bank%d" % i) for i in range(BANKS)]
+        groups = []
 
         def next_bank(width):
-            turn.append(width)
-            return banks[(len(turn) - 1) % 8][:, 0:width]
+            groups.append(width)
+            return banks[(len(groups) - 1) % BANKS][:, 0:width]
 
-        H = CH // 2
-        units = [(0, CH, 0), (CH, CH, 0), (2 * CH, 2 * CH, 0), (0, 2 * CH, 1), (2 * CH, CH, 1), (3 * CH, H, 1), (3 * CH + H, H, 1)]
-        pieces = [(0, CH), (CH, CH), (2 * CH, CH), (3 * CH, H), (3 * CH + H, H)]
-        squares, signed, woven, hq = {}, {}, {}, {}
+        narrow = CHUNK // 2
+        units = [(0, CHUNK, 0), (CHUNK, CHUNK, 0), (2 * CHUNK, 2 * CHUNK, 0)]
+        units = units + [(0, 2 * CHUNK, 1), (2 * CHUNK, CHUNK, 1), (3 * CHUNK, narrow, 1), (3 * CHUNK + narrow, narrow, 1)]
+        pieces = [(0, CHUNK), (CHUNK, CHUNK), (2 * CHUNK, CHUNK), (3 * CHUNK, narrow), (3 * CHUNK + narrow, narrow)]
+        squares, woven, h_quantised = {}, {}, {}
 
-        def stage1(u):
+        def first_product(u):
             j0, width, a = units[u]
             squares[u] = keep.tile([P, PACK, width], BF16, name="squares%d" % u, align_bytes=64)
-            run = min(width, CH)
-            for t in range(PACK):
+            run = min(width, CHUNK)
+            if a == 0:
+                order = [(t, s) for s in range(0, width, run) for t in range(PACK)]
+            else:
+                order = [(t, s) for t in range(PACK) for s in range(0, width, run)]
+            for t, s in order:
                 cols = slice(t * P, (t + 1) * P)
-                scols = slice(a * KP + t * P, a * KP + (t + 1) * P)
-                col = a * PACK + t
-                for s in range(0, width, run):
-                    c, start = divmod(j0 + s, CH)
-                    js = slice(start, start + run)
-                    bank = next_bank(run)
-                    nc.tensor.matmul_mx(
-                        out=bank, lhsT=wa_codes[a][:, cols].bitcast(FP8X4), lhsT_scale=wa_scales[a][:, cols],
-                        rhs=picked[("w1", c)][:, js].bitcast(FP8X4), rhs_scale=picked[("s1", c)][:, js], start=True, stop=False,
-                    )
-                    nc.tensor.matmul_mx(
-                        out=bank, lhsT=wb_codes[a][:, cols].bitcast(FP8X4), lhsT_scale=wbs[WB_ROW:P, scols],
-                        rhs=picked[("w2", c)][:, js].bitcast(FP8X4), rhs_scale=picked[("s2", c)][TAB2_ROW:P, js], start=False, stop=True,
-                    )
-                    nc.scalar.activation(out=squares[u][:, t, s : s + run], in_=bank, func=ACT.Square, scale=root[:, col : col + 1])
+                wb_s_cols = slice(a * PASS + t * P, a * PASS + (t + 1) * P)
+                factor = a * PACK + t
+                c, start = divmod(j0 + s, CHUNK)
+                js = slice(start, start + run)
+                bank = next_bank(run)
+                nc.tensor.matmul_mx(
+                    out=bank,
+                    lhsT=wa_codes[a][:, cols].bitcast(FP8X4),
+                    lhsT_scale=wa_s[a][:, cols],
+                    rhs=picked[("w1", c)][:, js].bitcast(FP8X4),
+                    rhs_scale=picked[("s1", c)][:, js],
+                    start=True,
+                    stop=False,
+                )
+                nc.tensor.matmul_mx(
+                    out=bank,
+                    lhsT=wb_codes[a][:, cols].bitcast(FP8X4),
+                    lhsT_scale=wb_s[WB_ROW:P, wb_s_cols],
+                    rhs=picked[("w2", c)][:, js].bitcast(FP8X4),
+                    rhs_scale=picked[("s2", c)][TAB2_ROW:P, js],
+                    start=False,
+                    stop=True,
+                )
+                nc.scalar.activation(out=squares[u][:, t, s : s + run], in_=bank, func=ACT.Square, scale=root[:, factor : factor + 1])
 
-        def signs(u):
-            j0, width, a = units[u]
-            signed[u] = keep.tile([P, PACK, width], BF16, name="signed%d" % u, tag="signed%d" % u, align_bytes=64)
-            for t in range(PACK):
-                col = a * PACK + t
-                nc.vector.tensor_scalar(signed[u][:, t, :], squares[u][:, t, :], sgn[:, col : col + 1], None, ALU.mult)
-
-        def weave(u):
-            width = units[u][1]
-            woven[u] = keep.tile([P, width, PACK], BF16, name="woven%d" % u, align_bytes=64)
-            nc.vector.tensor_copy(
-                out=woven[u][:].rearrange("p (g i) t -> p g t i", i=4),
-                in_=signed[u][:].rearrange("p t (g i) -> p g t i", i=4),
-            )
-
-        def sign_and_weave_on_gpsimd(u):
+        def sign_and_weave(u):
             j0, width, a = units[u]
             woven[u] = keep.tile([P, width, PACK], BF16, name="woven%d" % u, align_bytes=64)
-            for s in range(0, width, P):
+            shared = GPSIMD_COLUMNS if u == 0 else 0
+            for s in range(0, shared, P):
                 nc.gpsimd.tensor_tensor(
                     woven[u][:, s : s + P, :],
                     squares[u][:, :, s : s + P].rearrange("p t j -> p j t"),
                     sgn[:, a * PACK : (a + 1) * PACK].unsqueeze(1).to_broadcast([P, P, PACK]),
                     ALU.mult,
                 )
+            signed = keep.tile([P, PACK, width - shared], BF16, name="signed%d" % u, tag="signed%d" % u, align_bytes=64)
+            for t in range(PACK):
+                factor = a * PACK + t
+                nc.vector.tensor_scalar(signed[:, t, :], squares[u][:, t, shared:width], sgn[:, factor : factor + 1], None, ALU.mult)
+            nc.vector.tensor_copy(
+                out=woven[u][:, shared:width, :].rearrange("p (g i) t -> p g t i", i=4),
+                in_=signed[:].rearrange("p t (g i) -> p g t i", i=4),
+            )
 
-        def quantise(u):
+        def quantise_h(u):
             j0, width, a = units[u]
             codes = keep.tile([P, width], U32, name="h_codes%d" % u, tag="signed1" if u == 0 else "codes%d" % u, align_bytes=64)
-            scales = keep.tile([P, width], U8, name="h_scales%d" % u, align_bytes=64)
+            scales = keep.tile([P, width], U8, name="h_s%d" % u, align_bytes=64)
             nc.vector.quantize_mx(out=codes[:].bitcast(FP8X4), scales=scales[:], in_=woven[u][:].rearrange("p j t -> p (j t)"))
             for s in range(0, width, P):
-                hq[(j0 + s, a)] = (codes, scales, s)
+                h_quantised[(j0 + s, a)] = (codes, scales, s)
 
-        def stage2(k):
-            j0, width = pieces[k]
-            run = CH if width == CH else P
-            for nt in range(NT):
-                ybank = next_bank(width)
+        def second_product(piece):
+            j0, width = pieces[piece]
+            run = CHUNK if width == CHUNK else P
+            for nt in range(N_TILES):
+                bank = next_bank(width)
                 for a in range(HALVES):
                     for s in range(0, width, run):
-                        codes, scales, at = hq[(j0 + s, a)]
+                        codes, scales, at = h_quantised[(j0 + s, a)]
                         nc.tensor.matmul_mx(
-                            out=ybank[:, s : s + run],
-                            lhsT=enw[:, a, 2 * nt * P : 2 * (nt + 1) * P].bitcast(FP4X4),
-                            lhsT_scale=ens[:, a, nt * P : (nt + 1) * P],
+                            out=bank[:, s : s + run],
+                            lhsT=en_w[:, a, 2 * nt * P : 2 * (nt + 1) * P].bitcast(FP4X4),
+                            lhsT_scale=en_s[:, a, nt * P : (nt + 1) * P],
                             rhs=codes[:, at : at + run].bitcast(FP8X4),
                             rhs_scale=scales[:, at : at + run],
                             start=(a == 0 and s == 0),
                             stop=(a == HALVES - 1 and s + run == width),
                         )
-                y = ring.tile([P, width], F32, name="y", bufs=6)
-                if k >= 3 and nt == NT - 1:
-                    nc.vector.tensor_scalar(y[:], ybank, b_t[:, nt : nt + 1], None, ALU.add)
+                y = ring.tile([P, width], F32, name="y")
+                if piece >= VECTOR_FROM_PIECE and nt == N_TILES - 1:
+                    nc.vector.tensor_scalar(y[:], bank, b_t[:, nt : nt + 1], None, ALU.add)
                 else:
-                    nc.scalar.activation(out=y[:], in_=ybank, func=ACT.Identity, bias=b_t[:, nt : nt + 1])
+                    nc.scalar.activation(out=y[:], in_=bank, func=ACT.Identity, bias=b_t[:, nt : nt + 1])
                 nc.sync.dma_start(out=out[nt * P : (nt + 1) * P, j0 : j0 + width], in_=y[:])
 
-        gather("s1", 0, NCH)
-        gather("s2", 0, NCH)
-        deal_wb_words(0)
-        deal_wb_scales()
-        prepare_wa(0)
-        gather("w1", 0, 1)
-        gather("w2", 0, 1)
-        deal_wb_words(1)
-        gather("w1", 1, NCH - 1)
-        gather("w2", 1, NCH - 1)
-
-        for kind in ("w1", "w2"):
-            gather(kind, NCH - 1, NCH)
+        s1_all = keep.tile([P, J], U8, name="s1_all", align_bytes=64)
+        s2_early = keep.tile([P, 3 * CHUNK], U8, name="s2_early", align_bytes=64)
+        w1_early = keep.tile([P, 2 * CHUNK], U32, name="w1_early", align_bytes=64)
+        w2_all = keep.tile([P, J], U32, name="w2_all", align_bytes=64)
+        w1_late = placed.tile([P, 2 * CHUNK], U32, name="w1_late", align_bytes=64, offset=at_w1_late)
+        s2_late = placed.tile([P, CHUNK], U8, name="s2_late", align_bytes=64, offset=at_s2_late)
+        deal_columns(wb_codes[0][:], wb_raw[0][:])
+        for a in range(HALVES):
+            deal_columns(wb_s[:, a * PASS : (a + 1) * PASS], wb_s_raw[:, a * PASS : (a + 1) * PASS])
+        gather("s1", 0, 4, s1_all[:])
+        gather("s2", 0, 3, s2_early[:])
+        quantise_wa(0)
+        gather("w1", 0, 2, w1_early[:])
+        gather("w2", 0, 1, w2_all[:, 0:CHUNK])
+        gather("w2", 1, 2, w2_all[:, CHUNK : 2 * CHUNK])
+        gather("w2", 2, 4, w2_all[:, 2 * CHUNK : J])
+        deal_columns(wb_codes[1][:], wb_raw[1][:])
+        gather("w1", 2, 3, w1_late[:, 0:CHUNK])
+        gather("w1", 3, 4, w1_late[:, CHUNK : 2 * CHUNK])
+        gather("s2", 3, 4, s2_late[:])
 
         for u in range(len(units)):
-            stage1(u)
+            first_product(u)
             if u == 0:
-                prepare_wa(1)
-                sign_and_weave_on_gpsimd(u)
-            else:
-                signs(u)
-                weave(u)
-                if u == 1:
-                    quantise(0)
-                quantise(u)
-        for k in range(len(pieces)):
-            stage2(k)
+                quantise_wa(1)
+            sign_and_weave(u)
+            if u == 1:
+                quantise_h(0)
+            if u >= 1:
+                quantise_h(u)
+        for piece in range(len(pieces)):
+            second_product(piece)

from contextlib import ExitStack

import concourse.mybir as mybir

K, L, R, N, T, J = 512, 512, 1024, 256, 4096, 2048
FLOPS = 2 * K * R * J + 2 * L * R * J + 2 * R * N * J

F32 = mybir.dt.float32
BF16 = mybir.dt.bfloat16
I32 = mybir.dt.int32
U32 = mybir.dt.uint32
U16 = mybir.dt.uint16
U8 = mybir.dt.uint8
FP8X4 = mybir.dt.float8_e4m3fn_x4
FP4X4 = mybir.dt.float4_e2m1fn_x4
ACT = mybir.ActivationFunctionType
ALU = mybir.AluOpType

P = 128
PACK = 4
PASS = P * PACK
HALVES = R // PASS
CHUNK = 512
LIST_COLS = CHUNK // 16
N_TILES = N // P
QUADRANTS = 4
BANKS = 8
TAB2_ROW = 4
WB_ROW = 8
GPSIMD_COLUMNS = 256
VECTOR_FROM_PIECE = 2
OUT_BUFS = 6


def tile_list_kg_sqd_bias_kernel(
    tc, tab_words, tab_scales, tab2_words, tab2_scales, wa, wb_words, wb_scales, sm, en_words, en_scales, b, offs, offs2, out
):
    nc = tc.nc
    with ExitStack() as ctx:
        lists = ctx.enter_context(tc.tile_pool(name="lists", bufs=1))
        keep = ctx.enter_context(tc.tile_pool(name="keep", bufs=1))
        placed = ctx.enter_context(tc.tile_pool(name="placed", bufs=1))
        ring = ctx.enter_context(tc.tile_pool(name="ring", bufs=OUT_BUFS))
        psum = ctx.enter_context(tc.psum_pool(name="psum", bufs=1))

        offs_t = lists.tile([P, J // 16], U16, name="offs_t")
        offs2_t = lists.tile([P, J // 16], U16, name="offs2_t")
        tab_s = keep.tile([P, T], U8, name="tab_s", align_bytes=64)
        tab2_s = keep.tile([P, T], U8, name="tab2_s", align_bytes=64)
        wb_s_raw = keep.tile([P, R], U8, name="wb_s_raw", align_bytes=64)
        en_s = keep.tile([P, HALVES, N], U8, name="en_s", align_bytes=64)

        word_bytes = 4
        wa_half_bytes = word_bytes * PACK * PASS
        at_tab2 = word_bytes * T
        at_wa = 2 * word_bytes * T
        at_wb0 = at_wa + HALVES * wa_half_bytes
        at_en = at_wb0 + word_bytes * PASS
        at_b = at_en + HALVES * 2 * N
        at_sm = at_b + 64
        at_w1_late = at_sm + 64
        at_s2_late = at_w1_late + word_bytes * 2 * CHUNK
        at_wb1 = at_s2_late - CHUNK

        zeros = placed.tile([P, at_wb1 // word_bytes + PASS], I32, name="zeros", offset=0)
        nc.gpsimd.memset(tab_s[:].bitcast(I32), 0)
        nc.vector.memset(tab2_s[:].bitcast(I32), 0)
        nc.vector.memset(zeros[:, 0:1], 0)
        nc.vector.tensor_copy(out=wb_s_raw[:].bitcast(I32), in_=zeros[:, 0:1].to_broadcast([P, R // word_bytes]))
        nc.gpsimd.memset(en_s[:].rearrange("p a n -> p (a n)").bitcast(I32), 0)

        wa_rows = wa.rearrange("(p i) r -> p i r", i=PACK)
        wb_flat = wb_words[0].rearrange("p r i -> p (r i)").bitcast(I32)
        tab_w = placed.tile([P, T], U32, name="tab_w", align_bytes=64, offset=0)
        tab2_w = placed.tile([P, T], U32, name="tab2_w", align_bytes=64, offset=at_tab2)
        wa_raw = [placed.tile([P, PACK, PASS], F32, name="wa_raw%d" % a, offset=at_wa + wa_half_bytes * a) for a in range(HALVES)]
        wb_raw = [placed.tile([P, PASS], I32, name="wb_raw%d" % a, offset=(at_wb0, at_wb1)[a]) for a in range(HALVES)]
        en_w = placed.tile([P, HALVES, 2 * N], U8, name="en_w", align_bytes=64, offset=at_en)
        b_t = placed.tile([P, N_TILES], F32, name="b_t", offset=at_b)
        sm_t = placed.tile([P, HALVES, PACK], F32, name="sm_t", offset=at_sm)

        def load_scale_rows(dst, first, rows):
            for q in range(QUADRANTS):
                nc.sync.dma_start(out=dst[32 * q + first : 32 * q + first + 4, :].bitcast(I32), in_=rows[4 * q : 4 * q + 4, :].bitcast(I32))

        nc.sync.dma_start(offs_t[:], offs)
        load_scale_rows(tab_s, 0, tab_scales[0])
        nc.sync.dma_start(offs2_t[:], offs2)
        nc.sync.dma_start(out=wa_raw[0][:], in_=wa_rows[:, :, 0:PASS])
        nc.sync.dma_start(out=sm_t[:], in_=sm.rearrange("(a p t) -> p a t", a=HALVES, t=PACK))
        load_scale_rows(tab2_s, TAB2_ROW, tab2_scales[0])
        nc.sync.dma_start(out=wb_raw[0][:], in_=wb_flat[:, 0:PASS])
        load_scale_rows(wb_s_raw, WB_ROW, wb_scales[0])
        nc.sync.dma_start(out=tab_w[:].bitcast(I32), in_=tab_words[0].rearrange("p t i -> p (t i)").bitcast(I32))
        nc.sync.dma_start(out=tab2_w[:].bitcast(I32), in_=tab2_words[0].rearrange("p t i -> p (t i)").bitcast(I32))
        nc.sync.dma_start(out=wb_raw[1][:], in_=wb_flat[:, PASS:R])
        nc.sync.dma_start(out=wa_raw[1][:], in_=wa_rows[:, :, PASS:R])
        nc.sync.dma_start(out=en_w[:].bitcast(I32), in_=en_words.rearrange("a p n -> p a n").bitcast(I32))
        for q in range(QUADRANTS):
            nc.sync.dma_start(
                out=en_s[32 * q : 32 * q + 4, :, :].bitcast(I32),
                in_=en_scales[:, 4 * q : 4 * q + 4, :].rearrange("a q n -> q a n").bitcast(I32),
            )
        with nc.allow_non_contiguous_dma(reason="one bias value a partition"):
            nc.sync.dma_start(out=b_t[:], in_=b.rearrange("(c p) -> p c", p=P))

        factors = HALVES * PACK
        sm_flat = sm_t[:].rearrange("p a t -> p (a t)")
        sgn = keep.tile([P, factors], F32, name="sgn")
        mag = keep.tile([P, factors], F32, name="mag")
        guess = keep.tile([P, factors], F32, name="guess")
        guess_sq = keep.tile([P, factors], F32, name="guess_sq")
        half_inv = keep.tile([P, factors], F32, name="half_inv")
        resid = keep.tile([P, factors], F32, name="resid")
        root = keep.tile([P, factors], F32, name="root")
        nc.scalar.activation(out=half_inv[:], in_=sm_flat, func=ACT.Abs_reciprocal_sqrt, scale=4.0)
        nc.scalar.activation(out=mag[:], in_=sm_flat, func=ACT.Abs)
        nc.scalar.activation(out=guess[:], in_=mag[:], func=ACT.Sqrt)
        nc.scalar.activation(out=sgn[:], in_=sm_flat, func=ACT.Sign)
        nc.scalar.activation(out=guess_sq[:], in_=guess[:], func=ACT.Square)
        nc.gpsimd.tensor_tensor(resid[:], mag[:], guess_sq[:], ALU.subtract)
        nc.gpsimd.tensor_scalar(half_inv[:], half_inv[:], 2.0**62, 1.0, ALU.min, ALU.mult)
        nc.gpsimd.tensor_tensor(resid[:], resid[:], half_inv[:], ALU.mult)
        nc.gpsimd.tensor_tensor(root[:], guess[:], resid[:], ALU.add)

        wa_codes = [keep.tile([P, PASS], U32, name="wa_codes%d" % a, align_bytes=64) for a in range(HALVES)]
        wa_s = [keep.tile([P, PASS], U8, name="wa_s%d" % a, align_bytes=64) for a in range(HALVES)]
        wb_codes = [keep.tile([P, PASS], I32, name="wb_codes%d" % a, align_bytes=64) for a in range(HALVES)]
        wb_s = keep.tile([P, R], U8, name="wb_s", align_bytes=64)

        def quantise_wa(a):
            wa_bf = keep.tile([P, PACK, P, PACK], BF16, name="wa_bf%d" % a, align_bytes=64)
            if a == 0:
                nc.scalar.activation(
                    out=wa_bf[:].rearrange("p t m i -> p m i t"),
                    in_=wa_raw[a][:].rearrange("p i (m t) -> p m i t", t=PACK),
                    func=ACT.Copy,
                    scale=-1.0,
                )
            else:
                dealt = wa_raw[a][:].rearrange("p i (m t) -> p t m i", t=PACK)
                for t in range(PACK):
                    nc.gpsimd.tensor_scalar(wa_bf[:, t, :, :], dealt[:, t, :, :], -1.0, 0.0, ALU.mult, ALU.add)
            nc.vector.quantize_mx(out=wa_codes[a][:].bitcast(FP8X4), scales=wa_s[a][:], in_=wa_bf[:].rearrange("p t m i -> p (t m i)"))

        def deal_columns(dst, src):
            nc.gpsimd.tensor_copy(out=dst.rearrange("p (t m) -> p t m", t=PACK), in_=src.rearrange("p (m t) -> p t m", t=PACK))

        picked = {}

        def gather(kind, c0, c1, dst):
            table, offsets = {"s1": (tab_s, offs_t), "s2": (tab2_s, offs2_t), "w1": (tab_w, offs_t), "w2": (tab2_w, offs2_t)}[kind]
            nc.vector.tensor_copy(dst, table[:].indirect(offsets[:, c0 * LIST_COLS : c1 * LIST_COLS]))
            for c in range(c0, c1):
                picked[(kind, c)] = dst[:, (c - c0) * CHUNK : (c - c0 + 1) * CHUNK]

        banks = [psum.tile([P, CHUNK], F32, name="bank%d" % i) for i in range(BANKS)]
        groups = []

        def next_bank(width):
            groups.append(width)
            return banks[(len(groups) - 1) % BANKS][:, 0:width]

        narrow = CHUNK // 2
        units = [(0, CHUNK, 0), (CHUNK, CHUNK, 0), (2 * CHUNK, 2 * CHUNK, 0)]
        units = units + [(0, 2 * CHUNK, 1), (2 * CHUNK, CHUNK, 1), (3 * CHUNK, narrow, 1), (3 * CHUNK + narrow, narrow, 1)]
        pieces = [(0, CHUNK), (CHUNK, CHUNK), (2 * CHUNK, CHUNK), (3 * CHUNK, narrow), (3 * CHUNK + narrow, narrow)]
        squares, woven, h_quantised = {}, {}, {}

        def first_product(u):
            j0, width, a = units[u]
            squares[u] = keep.tile([P, PACK, width], BF16, name="squares%d" % u, align_bytes=64)
            run = min(width, CHUNK)
            if a == 0:
                order = [(t, s) for s in range(0, width, run) for t in range(PACK)]
            else:
                order = [(t, s) for t in range(PACK) for s in range(0, width, run)]
            for t, s in order:
                cols = slice(t * P, (t + 1) * P)
                wb_s_cols = slice(a * PASS + t * P, a * PASS + (t + 1) * P)
                factor = a * PACK + t
                c, start = divmod(j0 + s, CHUNK)
                js = slice(start, start + run)
                bank = next_bank(run)
                nc.tensor.matmul_mx(
                    out=bank,
                    lhsT=wa_codes[a][:, cols].bitcast(FP8X4),
                    lhsT_scale=wa_s[a][:, cols],
                    rhs=picked[("w1", c)][:, js].bitcast(FP8X4),
                    rhs_scale=picked[("s1", c)][:, js],
                    start=True,
                    stop=False,
                )
                nc.tensor.matmul_mx(
                    out=bank,
                    lhsT=wb_codes[a][:, cols].bitcast(FP8X4),
                    lhsT_scale=wb_s[WB_ROW:P, wb_s_cols],
                    rhs=picked[("w2", c)][:, js].bitcast(FP8X4),
                    rhs_scale=picked[("s2", c)][TAB2_ROW:P, js],
                    start=False,
                    stop=True,
                )
                nc.scalar.activation(out=squares[u][:, t, s : s + run], in_=bank, func=ACT.Square, scale=root[:, factor : factor + 1])

        def sign_and_weave(u):
            j0, width, a = units[u]
            woven[u] = keep.tile([P, width, PACK], BF16, name="woven%d" % u, align_bytes=64)
            shared = GPSIMD_COLUMNS if u == 0 else 0
            for s in range(0, shared, P):
                nc.gpsimd.tensor_tensor(
                    woven[u][:, s : s + P, :],
                    squares[u][:, :, s : s + P].rearrange("p t j -> p j t"),
                    sgn[:, a * PACK : (a + 1) * PACK].unsqueeze(1).to_broadcast([P, P, PACK]),
                    ALU.mult,
                )
            signed = keep.tile([P, PACK, width - shared], BF16, name="signed%d" % u, tag="signed%d" % u, align_bytes=64)
            for t in range(PACK):
                factor = a * PACK + t
                nc.vector.tensor_scalar(signed[:, t, :], squares[u][:, t, shared:width], sgn[:, factor : factor + 1], None, ALU.mult)
            nc.vector.tensor_copy(
                out=woven[u][:, shared:width, :].rearrange("p (g i) t -> p g t i", i=4),
                in_=signed[:].rearrange("p t (g i) -> p g t i", i=4),
            )

        def quantise_h(u):
            j0, width, a = units[u]
            codes = keep.tile([P, width], U32, name="h_codes%d" % u, tag="signed1" if u == 0 else "codes%d" % u, align_bytes=64)
            scales = keep.tile([P, width], U8, name="h_s%d" % u, align_bytes=64)
            nc.vector.quantize_mx(out=codes[:].bitcast(FP8X4), scales=scales[:], in_=woven[u][:].rearrange("p j t -> p (j t)"))
            for s in range(0, width, P):
                h_quantised[(j0 + s, a)] = (codes, scales, s)

        def second_product(piece):
            j0, width = pieces[piece]
            run = CHUNK if width == CHUNK else P
            for nt in range(N_TILES):
                bank = next_bank(width)
                for a in range(HALVES):
                    for s in range(0, width, run):
                        codes, scales, at = h_quantised[(j0 + s, a)]
                        nc.tensor.matmul_mx(
                            out=bank[:, s : s + run],
                            lhsT=en_w[:, a, 2 * nt * P : 2 * (nt + 1) * P].bitcast(FP4X4),
                            lhsT_scale=en_s[:, a, nt * P : (nt + 1) * P],
                            rhs=codes[:, at : at + run].bitcast(FP8X4),
                            rhs_scale=scales[:, at : at + run],
                            start=(a == 0 and s == 0),
                            stop=(a == HALVES - 1 and s + run == width),
                        )
                y = ring.tile([P, width], F32, name="y")
                if piece >= VECTOR_FROM_PIECE and nt == N_TILES - 1:
                    nc.vector.tensor_scalar(y[:], bank, b_t[:, nt : nt + 1], None, ALU.add)
                else:
                    nc.scalar.activation(out=y[:], in_=bank, func=ACT.Identity, bias=b_t[:, nt : nt + 1])
                nc.sync.dma_start(out=out[nt * P : (nt + 1) * P, j0 : j0 + width], in_=y[:])

        s1_all = keep.tile([P, J], U8, name="s1_all", align_bytes=64)
        s2_early = keep.tile([P, 3 * CHUNK], U8, name="s2_early", align_bytes=64)
        w1_early = keep.tile([P, 2 * CHUNK], U32, name="w1_early", align_bytes=64)
        w2_all = keep.tile([P, J], U32, name="w2_all", align_bytes=64)
        w1_late = placed.tile([P, 2 * CHUNK], U32, name="w1_late", align_bytes=64, offset=at_w1_late)
        s2_late = placed.tile([P, CHUNK], U8, name="s2_late", align_bytes=64, offset=at_s2_late)
        deal_columns(wb_codes[0][:], wb_raw[0][:])
        for a in range(HALVES):
            deal_columns(wb_s[:, a * PASS : (a + 1) * PASS], wb_s_raw[:, a * PASS : (a + 1) * PASS])
        gather("s1", 0, 4, s1_all[:])
        gather("s2", 0, 3, s2_early[:])
        quantise_wa(0)
        gather("w1", 0, 2, w1_early[:])
        gather("w2", 0, 1, w2_all[:, 0:CHUNK])
        gather("w2", 1, 2, w2_all[:, CHUNK : 2 * CHUNK])
        gather("w2", 2, 4, w2_all[:, 2 * CHUNK : J])
        deal_columns(wb_codes[1][:], wb_raw[1][:])
        gather("w1", 2, 3, w1_late[:, 0:CHUNK])
        gather("w1", 3, 4, w1_late[:, CHUNK : 2 * CHUNK])
        gather("s2", 3, 4, s2_late[:])

        for u in range(len(units)):
            first_product(u)
            if u == 0:
                quantise_wa(1)
            sign_and_weave(u)
            if u == 1:
                quantise_h(0)
            if u >= 1:
                quantise_h(u)
        for piece in range(len(pieces)):
            second_product(piece)
